import numpy as np
import ml_dtypes


def mxq(x, axis, fmt="e4m3"):
    dtype, down = {"e4m3": (ml_dtypes.float8_e4m3fn, 7), "e5m2": (ml_dtypes.float8_e5m2, 14)}[fmt]
    v = np.moveaxis(np.asarray(x, np.float32).astype(ml_dtypes.bfloat16).astype(np.float64), axis, -1)
    blocks = v.reshape(v.shape[:-1] + (-1, 32))
    amax = np.abs(blocks).max(-1, keepdims=True)
    byte = np.maximum(np.where(amax > 0, np.frexp(amax)[1] - 1 + 127, 0) - down, 1)
    scale = np.exp2(byte - 127.0)
    codes = (blocks / scale).astype(np.float32).astype(dtype).astype(np.float64)
    return np.moveaxis((codes * scale).reshape(v.shape), -1, axis)


WIDE = False


def mx_kscale(k):
    if not WIDE:
        return np.ones(k)
    levels = np.array([10, -10, 5, -5, 0])
    if k % 512:
        return np.exp2(np.random.permutation(np.resize(levels, k // 32))).repeat(32)
    a = np.empty((k // 512, 16))
    for p in range(k // 512):
        a[p, :8] = np.random.permutation(np.resize(levels, 8))
        for g in range(8):
            far = levels[np.abs(levels - a[p, g]) >= 10]
            a[p, g + 8] = far[np.random.randint(len(far))]
    return np.exp2(a.ravel()).repeat(32)


def f64(x):
    return np.asarray(x).astype(np.float64)


def striped(idx):
    return np.tile(idx.reshape(-1, 16).T, (8, 1)).astype(np.uint16)


def unstriped(offs):
    return offs[:16].T.reshape(-1).astype(np.int64)


E2M1 = np.array([0.0, 0.5, 1.0, 1.5, 2.0, 3.0, 4.0, 6.0, -0.0, -0.5, -1.0, -1.5, -2.0, -3.0, -4.0, -6.0])


def pack_weight(w, fmt):
    k, n = w.shape
    w = f64(np.asarray(w, np.float32).astype(ml_dtypes.bfloat16)).reshape(k // 32, 32, n)
    amax = np.abs(w).max(1)
    if fmt == "e4m3":
        byte = np.frexp(amax)[1] - 1 + 127 - 7
    else:
        mant, ex = np.frexp(amax / 6.0)
        byte = np.where(mant > 0.5, ex, ex - 1) + 127
    byte = np.clip(np.where(amax > 0, byte, 1), 1, 254)
    scaled = (w * np.exp2(127.0 - byte)[:, None, :]).reshape(k, n).astype(np.float32)
    by_word = np.ascontiguousarray(scaled.reshape(k // 512, 128, 4, n).transpose(0, 1, 3, 2))
    if fmt == "e4m3":
        words = by_word.astype(ml_dtypes.float8_e4m3fn).view(np.uint8)
    else:
        c = by_word.astype(ml_dtypes.float4_e2m1fn).view(np.uint8) & 0xF
        words = (c[..., 0::2] | (c[..., 1::2] << 4)).reshape(k // 512, 128, 2 * n)
    return np.ascontiguousarray(words), np.ascontiguousarray(byte.astype(np.uint8).reshape(k // 512, 16, n))


def unpack_weight(words, scales, fmt):
    g, _, n = scales.shape
    words = np.ascontiguousarray(words).reshape(g, 128, n, -1)
    if fmt == "e4m3":
        vals = words.view(ml_dtypes.float8_e4m3fn).astype(np.float64)
    else:
        nib = np.empty((g, 128, n, 4), np.uint8)
        nib[..., 0::2] = words & 0xF
        nib[..., 1::2] = words >> 4
        vals = E2M1[nib]
    vals = vals * np.repeat(np.exp2(scales.astype(np.float64) - 127.0), 8, axis=1)[..., None]
    return vals.transpose(0, 1, 3, 2).reshape(g * 512, n)


def gelu(v):
    return 0.5 * v * (1.0 + np.tanh(np.sqrt(2.0 / np.pi) * (v + 0.044715 * v**3)))


def striped8(idx):
    return np.concatenate([v.reshape(-1, 16).T for v in idx]).astype(np.uint16)


def unstriped8(offs):
    return np.stack([offs[16 * g:16 * g + 16].T.reshape(-1) for g in range(8)]).astype(np.int64)


def runs(v, idx8):
    k = np.arange(v.shape[0])
    return v[k[:, None], idx8[k % 512 // 64]]


def often(T, S):
    return np.random.permutation(T)[(T * np.random.uniform(0, 1, S) ** 4).astype(np.int64)]


K, H, N, T, S = 1024, 512, 256, 2048, 1024

def setup_inputs():
    n = np.random.standard_normal
    s = mx_kscale(K)[:, None]
    u = mx_kscale(H)[:, None]
    tab_words, tab_scales = pack_weight(n((K, T)) * s, "e4m3")
    offs = striped8(np.stack([often(T, S) for _ in range(8)]))
    w1 = (n((K, H)) / np.sqrt(K) / s).astype(np.float32)
    w2_words, w2_scales = pack_weight(n((K, H)) / np.sqrt(K) / s, "e2m1")
    w3_words, w3_scales = pack_weight(n((K, H)) / np.sqrt(K) / s, "e4m3")
    gain1 = (np.random.uniform(0.5, 1.5, H) * u[:, 0]).astype(np.float32)
    gain2 = (np.random.uniform(0.5, 1.5, H) * u[:, 0]).astype(np.float32)
    gain3 = (np.random.uniform(0.5, 1.5, H) * u[:, 0]).astype(np.float32)
    w4 = (1.5 * n((H, N)) / np.sqrt(H) / u).astype(np.float32)
    w5 = (1.5 * n((H, N)) / np.sqrt(H) / u).astype(np.float32)
    w6_words, w6_scales = pack_weight(1.5 * n((H, N)) / np.sqrt(H) / u, "e2m1")
    return {"tab_words": tab_words, "tab_scales": tab_scales, "offs": offs, "w1": w1,
            "w2_words": w2_words, "w2_scales": w2_scales, "w3_words": w3_words, "w3_scales": w3_scales,
            "gain1": gain1, "gain2": gain2, "gain3": gain3, "w4": w4, "w5": w5,
            "w6_words": w6_words, "w6_scales": w6_scales}

def reference(tab_words, tab_scales, offs, w1, w2_words, w2_scales, w3_words, w3_scales,
              gain1, gain2, gain3, w4, w5, w6_words, w6_scales):
    v = runs(unpack_weight(tab_words, tab_scales, "e4m3"), unstriped8(offs))
    h1 = mxq(f64(w1), 0, "e4m3").T @ v
    h2 = unpack_weight(w2_words, w2_scales, "e2m1").T @ v
    h3 = unpack_weight(w3_words, w3_scales, "e4m3").T @ v
    gain = np.concatenate([f64(gain1), f64(gain2), f64(gain3)])[:, None]
    act = gain * np.tanh(np.concatenate([h1, h2, h3], axis=0))
    q = mxq(act, 0, "e4m3")
    y1 = mxq(f64(w4), 0, "e4m3").T @ q[:H]
    y2 = mxq(f64(w5), 0, "e4m3").T @ q[H:2 * H]
    y3 = unpack_weight(w6_words, w6_scales, "e2m1").T @ q[2 * H:]
    return y1 * y2 + y3

@@ -1,0 +1,319 @@
+from contextlib import ExitStack
+
+import concourse.mybir as mybir
+
+K, H, N, T, S = 1024, 512, 256, 2048, 1024
+FLOPS = 2 * 3 * S * (K * H + H * N)
+
+F32 = mybir.dt.float32
+BF16 = mybir.dt.bfloat16
+I32 = mybir.dt.int32
+U32 = mybir.dt.uint32
+U16 = mybir.dt.uint16
+U8 = mybir.dt.uint8
+E4M3 = mybir.dt.float8_e4m3fn_x4
+E2M1 = mybir.dt.float4_e2m1fn_x4
+TANH = mybir.ActivationFunctionType.Tanh
+MULT = mybir.AluOpType.mult
+ADD = mybir.AluOpType.add
+
+P = 128
+PACK = 4
+PASSES = K // (P * PACK)
+CHUNK = 128
+PIECE = 256
+PIECES = S // PIECE
+HALVES = N // P
+
+
+def tile_list_land_air_exchange_kernel(
+    tc, tab_words, tab_scales, offs, w1, w2_words, w2_scales, w3_words, w3_scales,
+    gain1, gain2, gain3, w4, w5, w6_words, w6_scales, out,
+):
+    nc = tc.nc
+    with ExitStack() as ctx:
+        keep = ctx.enter_context(tc.tile_pool(name="keep", bufs=1))
+        ring = ctx.enter_context(tc.tile_pool(name="ring", bufs=4))
+        psum = ctx.enter_context(tc.psum_pool(name="psum", bufs=4))
+
+        def held(shape, dtype, name, tag=None):
+            return keep.tile(shape, dtype, name=name, tag=tag or name, align_bytes=64)
+
+        offsets = keep.tile([P, S // 16], U16, name="offsets")
+        nc.sync.dma_start(offsets[:], offs)
+
+        scale_window = held([P, T], U8, "scale_window", "reuse_a")
+        for a in range(PASSES):
+            nc.sync.dma_start(
+                scale_window[a:P:PASSES, :].bitcast(I32),
+                tab_scales[a].bitcast(I32).unsqueeze(1).to_broadcast([16, 4, T // 4]),
+            )
+        word_window = [held([P, T], U32, "word_window%d" % a, "reuse_w%d" % a) for a in range(PASSES)]
+        w2_raw = held([P, PASSES * H * 2], U8, "w2_raw", "reuse_b")
+        nc.sync.dma_start(word_window[0][:].bitcast(I32), tab_words[0].rearrange("p t i -> p (t i)").bitcast(I32))
+        gains = {name: held([P, PACK], F32, "gain_" + name) for name in ("h1", "h3")}
+        gains["h2"] = held([P, 8 * PACK], F32, "gain_h2_raw")
+        with nc.allow_non_contiguous_dma(reason="one gain for each partition and slot"):
+            for t in range(PACK):
+                nc.scalar.dma_start(
+                    gains["h2"][:, 8 * t : 8 * t + 1], gain2.rearrange("(b t i) -> t b i", t=PACK, i=8)[t].unsqueeze(2)
+                )
+        nc.sync.dma_start(
+            w2_raw[:].bitcast(I32).rearrange("p (a c) -> p a c", a=PASSES),
+            w2_words.bitcast(I32).rearrange("a p c -> p a c"),
+        )
+        nc.sync.dma_start(word_window[1][:].bitcast(I32), tab_words[1].rearrange("p t i -> p (t i)").bitcast(I32))
+
+        w2_scale_raw = held([P, PASSES * H], U8, "w2_scale_raw")
+        w3_scale_raw = held([P, H], U8, "w3_scale_raw")
+        w6_scale = held([P, N], U8, "w6_scale")
+        v_scale = held([P, PASSES * S], U8, "v_scale")
+        for plane in (w2_scale_raw, w3_scale_raw, w6_scale, v_scale):
+            nc.vector.memset(plane[:].bitcast(I32), 0)
+        for d in range(4):
+            nc.scalar.dma_start(
+                w2_scale_raw[32 * d : 32 * d + 4, :].bitcast(I32).rearrange("p (a c) -> p a c", a=PASSES),
+                w2_scales[:, 4 * d : 4 * d + 4, :].bitcast(I32).rearrange("a r c -> r a c"),
+            )
+        for d in range(4):
+            nc.gpsimd.dma_start(
+                w3_scale_raw[32 * d : 32 * d + 4 * PASSES, :].bitcast(I32),
+                w3_scales[:, 4 * d : 4 * d + 4, :].bitcast(I32),
+            )
+        for name, gain in (("h3", gain3), ("h1", gain1)):
+            nc.gpsimd.dma_start(gains[name][:], gain.rearrange("(p t) -> p t", t=PACK))
+        for d in range(4):
+            nc.gpsimd.dma_start(
+                w6_scale[32 * d : 32 * d + 4, :].bitcast(I32), w6_scales[0, 4 * d : 4 * d + 4, :].bitcast(I32)
+            )
+        w6_codes = held([P, 2 * N], U8, "w6_codes")
+        nc.gpsimd.dma_start(w6_codes[:].bitcast(I32), w6_words[0].bitcast(I32))
+
+        warm = held([P, 2], F32, "warm")
+        nc.vector.memset(warm[:, 0:1], 0.0)
+        nc.scalar.activation(warm[:, 1:2], warm[:, 0:1], TANH)
+
+        picked_scale = held([P, S], U8, "picked_scale", "reuse_c")
+        nc.vector.tensor_copy(picked_scale[:], scale_window[:].indirect(offsets[:]))
+        for a in range(PASSES):
+            for r in range(4):
+                (nc.scalar, nc.sync)[a].dma_start(
+                    v_scale[r:P:32, a * S : (a + 1) * S].bitcast(I32),
+                    picked_scale[8 * r + a : P : 32, :].bitcast(I32),
+                )
+        v_codes = [held([P, S], U32, "v_codes%d" % a) for a in range(PASSES)]
+
+        def gather_words(a, j0, j1):
+            nc.vector.tensor_copy(v_codes[a][:, j0:j1], word_window[a][:].indirect(offsets[:, j0 // 16 : j1 // 16]))
+
+        gather_words(0, 0, S)
+        gain_h2 = held([P, PACK], F32, "gain_h2")
+        nc.scalar.copy(gain_h2[:], gains["h2"][:, 0 : 8 * PACK : 8])
+        gains["h2"] = gain_h2
+
+        w2_codes = held([P, PASSES * H * 2], U8, "w2_codes")
+        w2_scale = held([P, PASSES * H], U8, "w2_scale")
+        nc.vector.tensor_copy(
+            w2_scale[:].bitcast(I32).rearrange("p (a t b w) -> p a t b w", a=PASSES, t=PACK, w=2),
+            w2_scale_raw[:].bitcast(I32).rearrange("p (a b t w) -> p a t b w", a=PASSES, t=PACK, w=2),
+        )
+        nc.vector.tensor_copy(
+            w2_codes[:].bitcast(I32).rearrange("p (a t b w) -> p a t b w", a=PASSES, t=PACK, w=4),
+            w2_raw[:].bitcast(I32).rearrange("p (a b t w) -> p a t b w", a=PASSES, t=PACK, w=4),
+        )
+        gather_words(1, 0, PIECE)
+        gather_words(1, PIECE, 2 * PIECE)
+        gather_words(1, 2 * PIECE, S)
+
+        w3_raw = held([P, PASSES * H], I32, "w3_raw", "reuse_a")
+        nc.sync.dma_start(
+            w3_raw[:].rearrange("p (a c) -> p a c", a=PASSES),
+            w3_words.rearrange("a p c i -> p a (c i)").bitcast(I32),
+        )
+        w1_raw = [held([P, PACK, H], F32, "w1_raw%d" % a, "reuse_w%d" % a) for a in range(PASSES)]
+        w5_raw = held([P, PACK, N], F32, "w5_raw", "reuse_b")
+        w4_raw = held([P, PACK, N], F32, "w4_raw", "reuse_c")
+        nc.sync.dma_start(w1_raw[0][:], w1[0 : P * PACK, :].rearrange("(p j) r -> p j r", j=PACK))
+        for t in range(PACK):
+            nc.sync.dma_start(w5_raw[:, t, :], w5.rearrange("(b t i) n -> t b i n", t=PACK, i=8)[t])
+        nc.sync.dma_start(w4_raw[:], w4.rearrange("(p t) n -> p t n", t=PACK))
+        nc.sync.dma_start(w1_raw[1][:], w1[P * PACK : K, :].rearrange("(p j) r -> p j r", j=PACK))
+
+        w3_codes = held([P, PASSES * H], I32, "w3_codes")
+        w3_scale = held([P, H], U8, "w3_scale")
+
+        def order_w3():
+            nc.vector.tensor_copy(
+                w3_scale[:].rearrange("p (t m) -> p m t", t=PACK), w3_scale_raw[:].rearrange("p (m t) -> p m t", t=PACK)
+            )
+            nc.vector.tensor_copy(
+                w3_codes[:].rearrange("p (a t m) -> p a m t", a=PASSES, t=PACK),
+                w3_raw[:].rearrange("p (a m t) -> p a m t", a=PASSES, t=PACK),
+            )
+
+        w1_round = [held([P, PACK, P, PACK], BF16, "w1_round%d" % a) for a in range(PASSES)]
+        w1_codes = held([P, PASSES * H], U32, "w1_codes")
+        w1_scale = held([P, PASSES * H], U8, "w1_scale")
+
+        def round_w1(a, half):
+            m0, m1 = half * P // 2, (half + 1) * P // 2
+            nc.scalar.copy(
+                w1_round[a][:, :, m0:m1, :].rearrange("p t m j -> p m j t"),
+                w1_raw[a][:, :, PACK * m0 : PACK * m1].rearrange("p j (m t) -> p m j t", t=PACK),
+            )
+
+        def quantize_w1(a):
+            nc.vector.quantize_mx(
+                w1_codes[:, a * H : (a + 1) * H].bitcast(E4M3),
+                w1_scale[:, a * H : (a + 1) * H],
+                w1_round[a][:].rearrange("p t m j -> p (t m j)"),
+            )
+
+        second = {}
+
+        def round_second(name, raw):
+            rounded = held([P, N, PACK], BF16, name + "_round")
+            nc.scalar.copy(
+                rounded[:].rearrange("p (c i) t -> p c t i", i=4), raw[:].rearrange("p t (c i) -> p c t i", i=4)
+            )
+            second[name] = rounded
+
+        def quantize_second(name):
+            codes = held([P, N], U32, name + "_codes")
+            scale = held([P, N], U8, name + "_scale")
+            nc.vector.quantize_mx(codes[:].bitcast(E4M3), scale[:], second[name][:].rearrange("p n t -> p (n t)"))
+            second[name] = (codes, scale)
+
+        def first_weight(name, a, t):
+            c0 = a * H + t * P
+            if name == "h1":
+                return w1_codes[:, c0 : c0 + P].bitcast(E4M3), w1_scale[:, c0 : c0 + P]
+            if name == "h2":
+                return w2_codes[:, 2 * c0 : 2 * (c0 + P)].bitcast(E2M1), w2_scale[:, c0 : c0 + P]
+            return w3_codes[:, c0 : c0 + P].bitcast(E4M3), w3_scale[4 * a : P, t * P : (t + 1) * P]
+
+        def second_weight(name, u):
+            if name == "h3":
+                return w6_codes[:, 2 * u * P : 2 * (u + 1) * P].bitcast(E2M1), w6_scale[:, u * P : (u + 1) * P]
+            codes, scale = second["w4" if name == "h1" else "w5"]
+            return codes[:, u * P : (u + 1) * P].bitcast(E4M3), scale[:, u * P : (u + 1) * P]
+
+        h_codes = {name: held([P, S], U32, name + "_codes") for name in gains}
+        h_scale = {name: held([P, S], U8, name + "_scale") for name in gains}
+        rounded_h = {}
+
+        def first_stage(name, piece):
+            start, width = piece
+            tanh = ring.tile([P, width, PACK], F32, name="tanh")
+            for c in range(width // CHUNK):
+                j0 = start + c * CHUNK
+                bank = psum.tile([P, PACK, CHUNK], F32, name="first_bank")
+                for t in range(PACK):
+                    for a in range(PASSES):
+                        codes, scale = first_weight(name, a, t)
+                        nc.tensor.matmul_mx(
+                            bank[:, t, :],
+                            lhsT=codes,
+                            lhsT_scale=scale,
+                            rhs=v_codes[a][:, j0 : j0 + CHUNK].bitcast(E4M3),
+                            rhs_scale=v_scale[:, a * S + j0 : a * S + j0 + CHUNK],
+                            start=(a == 0),
+                            stop=(a == PASSES - 1),
+                        )
+                nc.scalar.activation(
+                    tanh[:, c * CHUNK : (c + 1) * CHUNK, :], bank[:].rearrange("p t j -> p j t"), TANH
+                )
+            rounded = ring.tile([P, width, PACK], BF16, name="rounded", align_bytes=64)
+            nc.vector.tensor_tensor(
+                rounded[:], tanh[:], gains[name][:].unsqueeze(1).to_broadcast([P, width, PACK]), MULT
+            )
+            rounded_h[name, piece] = rounded
+
+        def quantize_h(name, piece):
+            cols = slice(piece[0], piece[0] + piece[1])
+            nc.vector.quantize_mx(
+                h_codes[name][:, cols].bitcast(E4M3),
+                h_scale[name][:, cols],
+                rounded_h[name, piece][:].rearrange("p j t -> p (j t)"),
+            )
+
+        def second_stage(name, piece):
+            cols = slice(piece[0], piece[0] + piece[1])
+            bank = psum.tile([P, HALVES, piece[1]], F32, name="second_bank")
+            for u in range(HALVES):
+                codes, scale = second_weight(name, u)
+                nc.tensor.matmul_mx(
+                    bank[:, u, :],
+                    lhsT=codes,
+                    lhsT_scale=scale,
+                    rhs=h_codes[name][:, cols].bitcast(E4M3),
+                    rhs_scale=h_scale[name][:, cols],
+                    start=True,
+                    stop=True,
+                )
+            return bank
+
+        y2 = held([P, HALVES, S], F32, "y2")
+
+        def park_y2(piece):
+            nc.scalar.copy(y2[:, :, piece[0] : piece[0] + piece[1]], second_stage("h2", piece)[:])
+
+        products = {}
+
+        def multiply(piece):
+            product = ring.tile([P, HALVES, piece[1]], F32, name="product")
+            nc.vector.tensor_tensor(
+                product[:], second_stage("h1", piece)[:], y2[:, :, piece[0] : piece[0] + piece[1]], MULT
+            )
+            products[piece] = product
+
+        def finish(piece):
+            result = ring.tile([P, HALVES, piece[1]], F32, name="result")
+            nc.vector.tensor_tensor(result[:], second_stage("h3", piece)[:], products[piece][:], ADD)
+            nc.sync.dma_start(
+                out.rearrange("(u p) j -> p u j", p=P)[:, :, piece[0] : piece[0] + piece[1]], result[:]
+            )
+
+        pieces = [(q * PIECE, PIECE) for q in range(PIECES)]
+        last = pieces[:-1] + [(S - PIECE, CHUNK), (S - CHUNK, CHUNK)]
+        for q in range(PIECES):
+            first_stage("h2", pieces[q])
+            if q == 0:
+                order_w3()
+            else:
+                quantize_h("h2", pieces[q - 1])
+            if q >= 2:
+                round_w1(0, q - 2)
+        for q in range(PIECES):
+            first_stage("h3", pieces[q])
+            quantize_h(*(("h3", pieces[q - 1]) if q else ("h2", pieces[-1])))
+            if q == 0:
+                quantize_w1(0)
+            if q in (1, 2):
+                round_w1(1, q - 1)
+        quantize_w1(1)
+        first_stage("h1", last[0])
+        round_second("w5", w5_raw)
+        quantize_h("h3", pieces[-1])
+        first_stage("h1", last[1])
+        round_second("w4", w4_raw)
+        quantize_h("h1", last[0])
+        quantize_second("w5")
+        park_y2(pieces[0])
+        first_stage("h1", last[2])
+        quantize_second("w4")
+        quantize_h("h1", last[1])
+        park_y2(pieces[1])
+        multiply(last[0])
+        for q in (3, 4):
+            first_stage("h1", last[q])
+            park_y2(pieces[q - 1])
+            quantize_h("h1", last[q - 1])
+            finish(last[q - 3])
+            multiply(last[q - 2])
+        quantize_h("h1", last[4])
+        finish(last[2])
+        multiply(last[3])
+        multiply(last[4])
+        finish(last[3])
+        finish(last[4])

@@ -1,6 +1,7 @@
 from contextlib import ExitStack
 
 import concourse.mybir as mybir
+from concourse.masks import make_identity
 
 K, H, N, T, S = 1024, 512, 256, 2048, 1024
 FLOPS = 2 * 3 * S * (K * H + H * N)
@@ -36,130 +37,152 @@ def tile_list_land_air_exchange_kernel(
         ring = ctx.enter_context(tc.tile_pool(name="ring", bufs=4))
         psum = ctx.enter_context(tc.psum_pool(name="psum", bufs=4))
 
-        def held(shape, dtype, name, tag=None):
-            return keep.tile(shape, dtype, name=name, tag=tag or name, align_bytes=64)
+        shared = ctx.enter_context(tc.tile_pool(name="shared", bufs=1))
+
+        def held(shape, dtype, name, at=None):
+            if at is None:
+                return keep.tile(shape, dtype, name=name, align_bytes=64)
+            return shared.tile(shape, dtype, name=name, align_bytes=64, offset=at)
 
         offsets = keep.tile([P, S // 16], U16, name="offsets")
         nc.sync.dma_start(offsets[:], offs)
 
-        scale_window = held([P, T], U8, "scale_window", "reuse_a")
+        scale_window = held([P, T], U8, "scale_window")
         for a in range(PASSES):
             nc.sync.dma_start(
                 scale_window[a:P:PASSES, :].bitcast(I32),
                 tab_scales[a].bitcast(I32).unsqueeze(1).to_broadcast([16, 4, T // 4]),
             )
-        word_window = [held([P, T], U32, "word_window%d" % a, "reuse_w%d" % a) for a in range(PASSES)]
-        w2_raw = held([P, PASSES * H * 2], U8, "w2_raw", "reuse_b")
-        nc.sync.dma_start(word_window[0][:].bitcast(I32), tab_words[0].rearrange("p t i -> p (t i)").bitcast(I32))
-        gains = {name: held([P, PACK], F32, "gain_" + name) for name in ("h1", "h3")}
-        gains["h2"] = held([P, 8 * PACK], F32, "gain_h2_raw")
-        with nc.allow_non_contiguous_dma(reason="one gain for each partition and slot"):
-            for t in range(PACK):
-                nc.scalar.dma_start(
-                    gains["h2"][:, 8 * t : 8 * t + 1], gain2.rearrange("(b t i) -> t b i", t=PACK, i=8)[t].unsqueeze(2)
-                )
+        word_window = [held([P, T], U32, "word_window%d" % a, 8192 * a) for a in range(PASSES)]
+        w2_raw = held([P, PASSES * H * 2], U8, "w2_raw", 20416)
+        w2_scale_raw = held([P, PASSES * H], U8, "w2_scale_raw")
+        gain2_rows = held([P, P], F32, "gain2_rows")
+        identity = held([P, P], F32, "identity")
+        v_scale = held([P, PASSES * S], U8, "v_scale")
+        nc.gpsimd.memset(w2_scale_raw[:].bitcast(I32), 0)
+        nc.gpsimd.memset(gain2_rows[:], 0.0)
+        make_identity(nc, identity[:])
+        nc.vector.memset(v_scale[:, S:].bitcast(I32), 0)
         nc.sync.dma_start(
             w2_raw[:].bitcast(I32).rearrange("p (a c) -> p a c", a=PASSES),
             w2_words.bitcast(I32).rearrange("a p c -> p a c"),
         )
-        nc.sync.dma_start(word_window[1][:].bitcast(I32), tab_words[1].rearrange("p t i -> p (t i)").bitcast(I32))
-
-        w2_scale_raw = held([P, PASSES * H], U8, "w2_scale_raw")
-        w3_scale_raw = held([P, H], U8, "w3_scale_raw")
-        w6_scale = held([P, N], U8, "w6_scale")
-        v_scale = held([P, PASSES * S], U8, "v_scale")
-        for plane in (w2_scale_raw, w3_scale_raw, w6_scale, v_scale):
-            nc.vector.memset(plane[:].bitcast(I32), 0)
+        nc.sync.dma_start(word_window[0][:].bitcast(I32), tab_words[0].rearrange("p t i -> p (t i)").bitcast(I32))
         for d in range(4):
-            nc.scalar.dma_start(
+            nc.sync.dma_start(
                 w2_scale_raw[32 * d : 32 * d + 4, :].bitcast(I32).rearrange("p (a c) -> p a c", a=PASSES),
                 w2_scales[:, 4 * d : 4 * d + 4, :].bitcast(I32).rearrange("a r c -> r a c"),
             )
-        for d in range(4):
-            nc.gpsimd.dma_start(
-                w3_scale_raw[32 * d : 32 * d + 4 * PASSES, :].bitcast(I32),
-                w3_scales[:, 4 * d : 4 * d + 4, :].bitcast(I32),
-            )
-        for name, gain in (("h3", gain3), ("h1", gain1)):
-            nc.gpsimd.dma_start(gains[name][:], gain.rearrange("(p t) -> p t", t=PACK))
-        for d in range(4):
-            nc.gpsimd.dma_start(
-                w6_scale[32 * d : 32 * d + 4, :].bitcast(I32), w6_scales[0, 4 * d : 4 * d + 4, :].bitcast(I32)
-            )
-        w6_codes = held([P, 2 * N], U8, "w6_codes")
-        nc.gpsimd.dma_start(w6_codes[:].bitcast(I32), w6_words[0].bitcast(I32))
+        nc.sync.dma_start(
+            gain2_rows[0:PACK, :].rearrange("t (b i) -> t b i", i=8), gain2.rearrange("(b t i) -> t b i", t=PACK, i=8)
+        )
+        nc.sync.dma_start(word_window[1][:].bitcast(I32), tab_words[1].rearrange("p t i -> p (t i)").bitcast(I32))
+        gains = {}
+
+        def load_gain_columns(queue, gain, run, name, at=None):
+            raw = held([P, 8 * PACK], F32, name, at)
+            with nc.allow_non_contiguous_dma(reason="one gain for each partition and slot"):
+                for t in range(PACK):
+                    queue.dma_start(
+                        raw[:, 8 * t : 8 * t + 1], gain.rearrange("(b t i) -> t b i", t=PACK, i=run)[t].unsqueeze(2)
+                    )
+            return raw
+
+        def pack_gain(name, raw):
+            gains[name] = held([P, PACK], F32, "gain_" + name)
+            nc.scalar.copy(gains[name][:], raw[:, 0 : 8 * PACK : 8])
+
+        gain2_bank = psum.tile([P, P], F32, name="second_bank")
+        nc.tensor.transpose(gain2_bank[:], gain2_rows[:], identity[:])
+        gains["h2"] = gain2_bank[:, 0:PACK]
 
         warm = held([P, 2], F32, "warm")
         nc.vector.memset(warm[:, 0:1], 0.0)
         nc.scalar.activation(warm[:, 1:2], warm[:, 0:1], TANH)
 
-        picked_scale = held([P, S], U8, "picked_scale", "reuse_c")
+        picked_scale = held([P, S], U8, "picked_scale", 34624)
         nc.vector.tensor_copy(picked_scale[:], scale_window[:].indirect(offsets[:]))
-        for a in range(PASSES):
-            for r in range(4):
-                (nc.scalar, nc.sync)[a].dma_start(
-                    v_scale[r:P:32, a * S : (a + 1) * S].bitcast(I32),
-                    picked_scale[8 * r + a : P : 32, :].bitcast(I32),
-                )
+        nc.vector.tensor_copy(v_scale[:, 0:S].bitcast(I32), picked_scale[:].bitcast(I32))
+        for a, r in [(1, 0), (1, 1), (1, 2), (1, 3), (0, 1), (0, 2), (0, 3)]:
+            nc.sync.dma_start(
+                v_scale[r:P:32, a * S : (a + 1) * S].bitcast(I32),
+                picked_scale[8 * r + a : P : 32, :].bitcast(I32),
+            )
         v_codes = [held([P, S], U32, "v_codes%d" % a) for a in range(PASSES)]
 
         def gather_words(a, j0, j1):
             nc.vector.tensor_copy(v_codes[a][:, j0:j1], word_window[a][:].indirect(offsets[:, j0 // 16 : j1 // 16]))
 
-        gather_words(0, 0, S)
-        gain_h2 = held([P, PACK], F32, "gain_h2")
-        nc.scalar.copy(gain_h2[:], gains["h2"][:, 0 : 8 * PACK : 8])
-        gains["h2"] = gain_h2
-
         w2_codes = held([P, PASSES * H * 2], U8, "w2_codes")
         w2_scale = held([P, PASSES * H], U8, "w2_scale")
-        nc.vector.tensor_copy(
-            w2_scale[:].bitcast(I32).rearrange("p (a t b w) -> p a t b w", a=PASSES, t=PACK, w=2),
-            w2_scale_raw[:].bitcast(I32).rearrange("p (a b t w) -> p a t b w", a=PASSES, t=PACK, w=2),
-        )
         nc.vector.tensor_copy(
             w2_codes[:].bitcast(I32).rearrange("p (a t b w) -> p a t b w", a=PASSES, t=PACK, w=4),
             w2_raw[:].bitcast(I32).rearrange("p (a b t w) -> p a t b w", a=PASSES, t=PACK, w=4),
         )
+        gather_words(0, 0, S)
+        nc.vector.tensor_copy(
+            w2_scale[:].bitcast(I32).rearrange("p (a t b w) -> p a t b w", a=PASSES, t=PACK, w=2),
+            w2_scale_raw[:].bitcast(I32).rearrange("p (a b t w) -> p a t b w", a=PASSES, t=PACK, w=2),
+        )
         gather_words(1, 0, PIECE)
-        gather_words(1, PIECE, 2 * PIECE)
-        gather_words(1, 2 * PIECE, S)
+        gather_words(1, PIECE, S)
 
-        w3_raw = held([P, PASSES * H], I32, "w3_raw", "reuse_a")
+        w1_raw = [held([P, PACK, H], F32, "w1_raw%d" % a, (22400, 0)[a]) for a in range(PASSES)]
+        w3_raw = held([P, PASSES * H], I32, "w3_raw", 16384)
+        w3_scale_raw = held([P, H], U8, "w3_scale_raw", 20480)
+        w6_scale = held([P, N], U8, "w6_scale", 34688)
+        w6_codes = held([P, 2 * N], U8, "w6_codes", 34944)
+        gains["h3"] = held([P, PACK], F32, "gain_h3", 21760)
+        w5_raw = held([P, PACK, N], F32, "w5_raw", 30592)
+        w4_raw = held([P, PACK, N], F32, "w4_raw", 35584)
+        for plane in (w3_scale_raw, w6_scale):
+            nc.gpsimd.memset(plane[:].bitcast(I32), 0)
+        w1_rows = w1.rearrange("(a p j) r -> a p j r", a=PASSES, j=PACK)
         nc.sync.dma_start(
             w3_raw[:].rearrange("p (a c) -> p a c", a=PASSES),
             w3_words.rearrange("a p c i -> p a (c i)").bitcast(I32),
         )
-        w1_raw = [held([P, PACK, H], F32, "w1_raw%d" % a, "reuse_w%d" % a) for a in range(PASSES)]
-        w5_raw = held([P, PACK, N], F32, "w5_raw", "reuse_b")
-        w4_raw = held([P, PACK, N], F32, "w4_raw", "reuse_c")
-        nc.sync.dma_start(w1_raw[0][:], w1[0 : P * PACK, :].rearrange("(p j) r -> p j r", j=PACK))
+        for d in range(4):
+            nc.sync.dma_start(
+                w3_scale_raw[32 * d : 32 * d + 4 * PASSES, :].bitcast(I32),
+                w3_scales[:, 4 * d : 4 * d + 4, :].bitcast(I32),
+            )
+        for a in range(PASSES):
+            nc.sync.dma_start(w1_raw[a][:], w1_rows[a])
+        nc.sync.dma_start(gains["h3"][:], gain3.rearrange("(p t) -> p t", t=PACK))
+        gain1_raw = load_gain_columns(nc.sync, gain1, 4, "gain1_raw", 35456)
         for t in range(PACK):
             nc.sync.dma_start(w5_raw[:, t, :], w5.rearrange("(b t i) n -> t b i n", t=PACK, i=8)[t])
-        nc.sync.dma_start(w4_raw[:], w4.rearrange("(p t) n -> p t n", t=PACK))
-        nc.sync.dma_start(w1_raw[1][:], w1[P * PACK : K, :].rearrange("(p j) r -> p j r", j=PACK))
+        for t in range(PACK):
+            nc.sync.dma_start(w4_raw[:, t, :], w4.rearrange("(e t i) n -> t e i n", t=PACK, i=4)[t])
+        nc.sync.dma_start(w6_codes[:].bitcast(I32), w6_words[0].bitcast(I32))
+        for d in range(4):
+            nc.sync.dma_start(
+                w6_scale[32 * d : 32 * d + 4, :].bitcast(I32), w6_scales[0, 4 * d : 4 * d + 4, :].bitcast(I32)
+            )
 
-        w3_codes = held([P, PASSES * H], I32, "w3_codes")
-        w3_scale = held([P, H], U8, "w3_scale")
+        w3_codes = held([P, PASSES * H], I32, "w3_codes", 39680)
+        w3_scale = held([P, H], U8, "w3_scale", 43776)
 
         def order_w3():
             nc.vector.tensor_copy(
-                w3_scale[:].rearrange("p (t m) -> p m t", t=PACK), w3_scale_raw[:].rearrange("p (m t) -> p m t", t=PACK)
-            )
-            nc.vector.tensor_copy(
                 w3_codes[:].rearrange("p (a t m) -> p a m t", a=PASSES, t=PACK),
                 w3_raw[:].rearrange("p (a m t) -> p a m t", a=PASSES, t=PACK),
+            )
+
+        def order_w3_scale():
+            nc.vector.tensor_copy(
+                w3_scale[:].rearrange("p (t m) -> p t m", t=PACK), w3_scale_raw[:].rearrange("p (m t) -> p t m", t=PACK)
             )
 
         w1_round = [held([P, PACK, P, PACK], BF16, "w1_round%d" % a) for a in range(PASSES)]
         w1_codes = held([P, PASSES * H], U32, "w1_codes")
         w1_scale = held([P, PASSES * H], U8, "w1_scale")
 
-        def round_w1(a, half):
-            m0, m1 = half * P // 2, (half + 1) * P // 2
+        def round_w1(a, t):
             nc.scalar.copy(
-                w1_round[a][:, :, m0:m1, :].rearrange("p t m j -> p m j t"),
-                w1_raw[a][:, :, PACK * m0 : PACK * m1].rearrange("p j (m t) -> p m j t", t=PACK),
+                w1_round[a][:, t].rearrange("p (e i) j -> p e j i", i=4),
+                w1_raw[a][:].rearrange("p j (e t i) -> p t e j i", t=PACK, i=4)[:, t],
             )
 
         def quantize_w1(a):
@@ -198,34 +221,49 @@ def tile_list_land_air_exchange_kernel(
             codes, scale = second["w4" if name == "h1" else "w5"]
             return codes[:, u * P : (u + 1) * P].bitcast(E4M3), scale[:, u * P : (u + 1) * P]
 
-        h_codes = {name: held([P, S], U32, name + "_codes") for name in gains}
-        h_scale = {name: held([P, S], U8, name + "_scale") for name in gains}
+        h_codes = {name: held([P, S], U32, name + "_codes") for name in ("h1", "h2", "h3")}
+        h_scale = {name: held([P, S], U8, name + "_scale") for name in ("h1", "h2", "h3")}
         rounded_h = {}
 
-        def first_stage(name, piece):
-            start, width = piece
-            tanh = ring.tile([P, width, PACK], F32, name="tanh")
-            for c in range(width // CHUNK):
-                j0 = start + c * CHUNK
-                bank = psum.tile([P, PACK, CHUNK], F32, name="first_bank")
-                for t in range(PACK):
-                    for a in range(PASSES):
-                        codes, scale = first_weight(name, a, t)
-                        nc.tensor.matmul_mx(
-                            bank[:, t, :],
-                            lhsT=codes,
-                            lhsT_scale=scale,
-                            rhs=v_codes[a][:, j0 : j0 + CHUNK].bitcast(E4M3),
-                            rhs_scale=v_scale[:, a * S + j0 : a * S + j0 + CHUNK],
-                            start=(a == 0),
-                            stop=(a == PASSES - 1),
-                        )
-                nc.scalar.activation(
-                    tanh[:, c * CHUNK : (c + 1) * CHUNK, :], bank[:].rearrange("p t j -> p j t"), TANH
+        banks = {}
+        tanhs = {}
+
+        def first_pass(name, chunk, a):
+            if a == 0:
+                banks[name, chunk] = psum.tile([P, PACK, CHUNK], F32, name="first_bank")
+            j0 = chunk * CHUNK
+            for t in range(PACK):
+                codes, scale = first_weight(name, a, t)
+                nc.tensor.matmul_mx(
+                    banks[name, chunk][:, t, :],
+                    lhsT=codes,
+                    lhsT_scale=scale,
+                    rhs=v_codes[a][:, j0 : j0 + CHUNK].bitcast(E4M3),
+                    rhs_scale=v_scale[:, a * S + j0 : a * S + j0 + CHUNK],
+                    start=(a == 0 and t == 0),
+                    stop=(a == PASSES - 1 and t == PACK - 1),
                 )
-            rounded = ring.tile([P, width, PACK], BF16, name="rounded", align_bytes=64)
+
+        def activate(name, chunk, piece):
+            start, width = piece
+            c0 = chunk * CHUNK - start
+            if c0 == 0:
+                if (name, chunk) == ("h2", 1):
+                    tanhs[name, piece] = held([P, width, PACK], F32, "tanh_early", 39680)
+                else:
+                    tanhs[name, piece] = ring.tile([P, width, PACK], F32, name="tanh")
+            nc.scalar.activation(
+                tanhs[name, piece][:, c0 : c0 + CHUNK, :], banks[name, chunk][:].rearrange("p t j -> p j t"), TANH
+            )
+
+        def apply_gain(name, piece):
+            width = piece[1]
+            if (name, piece) == ("h2", (CHUNK, CHUNK)):
+                rounded = held([P, width, PACK], BF16, "rounded_early", 43776)
+            else:
+                rounded = ring.tile([P, width, PACK], BF16, name="rounded", align_bytes=64)
             nc.vector.tensor_tensor(
-                rounded[:], tanh[:], gains[name][:].unsqueeze(1).to_broadcast([P, width, PACK]), MULT
+                rounded[:], tanhs[name, piece][:], gains[name][:].unsqueeze(1).to_broadcast([P, width, PACK]), MULT
             )
             rounded_h[name, piece] = rounded
 
@@ -274,46 +312,49 @@ def tile_list_land_air_exchange_kernel(
                 out.rearrange("(u p) j -> p u j", p=P)[:, :, piece[0] : piece[0] + piece[1]], result[:]
             )
 
-        pieces = [(q * PIECE, PIECE) for q in range(PIECES)]
-        last = pieces[:-1] + [(S - PIECE, CHUNK), (S - CHUNK, CHUNK)]
-        for q in range(PIECES):
-            first_stage("h2", pieces[q])
-            if q == 0:
-                order_w3()
-            else:
-                quantize_h("h2", pieces[q - 1])
-            if q >= 2:
-                round_w1(0, q - 2)
-        for q in range(PIECES):
-            first_stage("h3", pieces[q])
-            quantize_h(*(("h3", pieces[q - 1]) if q else ("h2", pieces[-1])))
-            if q == 0:
-                quantize_w1(0)
-            if q in (1, 2):
-                round_w1(1, q - 1)
-        quantize_w1(1)
-        first_stage("h1", last[0])
-        round_second("w5", w5_raw)
-        quantize_h("h3", pieces[-1])
-        first_stage("h1", last[1])
-        round_second("w4", w4_raw)
-        quantize_h("h1", last[0])
-        quantize_second("w5")
-        park_y2(pieces[0])
-        first_stage("h1", last[2])
-        quantize_second("w4")
-        quantize_h("h1", last[1])
-        park_y2(pieces[1])
-        multiply(last[0])
-        for q in (3, 4):
-            first_stage("h1", last[q])
-            park_y2(pieces[q - 1])
-            quantize_h("h1", last[q - 1])
-            finish(last[q - 3])
-            multiply(last[q - 2])
+        def cut(widths):
+            return [(sum(widths[:i]), w) for i, w in enumerate(widths)]
+
+        pieces = {"h2": cut([128, 128, 256, 512]), "h3": cut([512, 512]), "h1": cut([256, 256, 256, 128, 128])}
+        quarters = cut([PIECE] * PIECES)
+        last = pieces["h1"]
+        chunks = S // CHUNK
+        after = {
+            ("h2", 1): [order_w3],
+            ("h2", 3): [order_w3_scale],
+            ("h2", 7): [lambda: quantize_w1(0)],
+            ("h3", 4): [lambda: quantize_w1(1), lambda: pack_gain("h1", gain1_raw)],
+            ("h1", 0): [lambda: round_second("w5", w5_raw)],
+            ("h1", 1): [lambda: quantize_second("w5"), lambda: round_second("w4", w4_raw)],
+            ("h1", 2): [lambda: park_y2(quarters[0]), lambda: quantize_second("w4")],
+            ("h1", 3): [lambda: park_y2(quarters[1]), lambda: multiply(last[0])],
+            ("h1", 5): [lambda: park_y2(quarters[2]), lambda: finish(last[0]), lambda: multiply(last[1])],
+            ("h1", 6): [lambda: park_y2(quarters[3]), lambda: finish(last[1]), lambda: multiply(last[2])],
+            ("h1", 7): [lambda: finish(last[2]), lambda: multiply(last[3])],
+        }
+        rounding = [(a, t) for a in range(PASSES) for t in range(PACK)]
+        waiting = []
+        for chunk in range(2):
+            first_pass("h2", chunk, 0)
+        step = 0
+        for name in ("h2", "h3", "h1"):
+            for piece in pieces[name]:
+                for chunk in range(piece[0] // CHUNK, (piece[0] + piece[1]) // CHUNK):
+                    if step >= 2:
+                        first_pass(name, chunk, 0)
+                    first_pass(name, chunk, 1)
+                    activate(name, chunk, piece)
+                    if 3 <= step < 3 + len(rounding):
+                        round_w1(*rounding[step - 3])
+                    if (chunk + 1) * CHUNK == piece[0] + piece[1]:
+                        apply_gain(name, piece)
+                        for earlier in waiting:
+                            quantize_h(*earlier)
+                        waiting = [(name, piece)]
+                    for call in after.get((name, chunk), []):
+                        call()
+                    step = step + 1
         quantize_h("h1", last[4])
-        finish(last[2])
-        multiply(last[3])
-        multiply(last[4])
         finish(last[3])
+        multiply(last[4])
         finish(last[4])

@@ -96,10 +96,6 @@ def tile_list_land_air_exchange_kernel(
         nc.tensor.transpose(gain2_bank[:], gain2_rows[:], identity[:])
         gains["h2"] = gain2_bank[:, 0:PACK]
 
-        warm = held([P, 2], F32, "warm")
-        nc.vector.memset(warm[:, 0:1], 0.0)
-        nc.scalar.activation(warm[:, 1:2], warm[:, 0:1], TANH)
-
         picked_scale = held([P, S], U8, "picked_scale", 34624)
         nc.vector.tensor_copy(picked_scale[:], scale_window[:].indirect(offsets[:]))
         nc.vector.tensor_copy(v_scale[:, 0:S].bitcast(I32), picked_scale[:].bitcast(I32))

@@ -22,9 +22,9 @@ P = 128
 PACK = 4
 PASSES = K // (P * PACK)
 CHUNK = 128
-PIECE = 256
-PIECES = S // PIECE
+QUARTER = 256
 HALVES = N // P
+GAIN_STEP = 16
 
 
 def tile_list_land_air_exchange_kernel(
@@ -35,8 +35,9 @@ def tile_list_land_air_exchange_kernel(
     with ExitStack() as ctx:
         keep = ctx.enter_context(tc.tile_pool(name="keep", bufs=1))
         ring = ctx.enter_context(tc.tile_pool(name="ring", bufs=4))
-        psum = ctx.enter_context(tc.psum_pool(name="psum", bufs=4))
-
+        first_banks = ctx.enter_context(tc.psum_pool(name="first_banks", bufs=4))
+        second_banks = ctx.enter_context(tc.psum_pool(name="second_banks", bufs=3))
+        gain_banks = ctx.enter_context(tc.psum_pool(name="gain_banks", bufs=1))
         shared = ctx.enter_context(tc.tile_pool(name="shared", bufs=1))
 
         def held(shape, dtype, name, at=None):
@@ -57,11 +58,13 @@ def tile_list_land_air_exchange_kernel(
         w2_raw = held([P, PASSES * H * 2], U8, "w2_raw", 20416)
         w2_scale_raw = held([P, PASSES * H], U8, "w2_scale_raw")
         gain2_rows = held([P, P], F32, "gain2_rows")
+        gain_rows = held([P, H], F32, "gain_rows")
         identity = held([P, P], F32, "identity")
         v_scale = held([P, PASSES * S], U8, "v_scale")
         nc.gpsimd.memset(w2_scale_raw[:].bitcast(I32), 0)
         nc.gpsimd.memset(gain2_rows[:], 0.0)
         make_identity(nc, identity[:])
+        nc.gpsimd.memset(gain_rows[:], 0.0)
         nc.vector.memset(v_scale[:, S:].bitcast(I32), 0)
         nc.sync.dma_start(
             w2_raw[:].bitcast(I32).rearrange("p (a c) -> p a c", a=PASSES),
@@ -77,24 +80,10 @@ def tile_list_land_air_exchange_kernel(
             gain2_rows[0:PACK, :].rearrange("t (b i) -> t b i", i=8), gain2.rearrange("(b t i) -> t b i", t=PACK, i=8)
         )
         nc.sync.dma_start(word_window[1][:].bitcast(I32), tab_words[1].rearrange("p t i -> p (t i)").bitcast(I32))
-        gains = {}
 
-        def load_gain_columns(queue, gain, run, name, at=None):
-            raw = held([P, 8 * PACK], F32, name, at)
-            with nc.allow_non_contiguous_dma(reason="one gain for each partition and slot"):
-                for t in range(PACK):
-                    queue.dma_start(
-                        raw[:, 8 * t : 8 * t + 1], gain.rearrange("(b t i) -> t b i", t=PACK, i=run)[t].unsqueeze(2)
-                    )
-            return raw
-
-        def pack_gain(name, raw):
-            gains[name] = held([P, PACK], F32, "gain_" + name)
-            nc.scalar.copy(gains[name][:], raw[:, 0 : 8 * PACK : 8])
-
-        gain2_bank = psum.tile([P, P], F32, name="second_bank")
+        gain2_bank = second_banks.tile([P, P], F32, name="second_bank")
         nc.tensor.transpose(gain2_bank[:], gain2_rows[:], identity[:])
-        gains["h2"] = gain2_bank[:, 0:PACK]
+        gains = {"h2": gain2_bank[:, 0:PACK]}
 
         picked_scale = held([P, S], U8, "picked_scale", 34624)
         nc.vector.tensor_copy(picked_scale[:], scale_window[:].indirect(offsets[:]))
@@ -120,15 +109,15 @@ def tile_list_land_air_exchange_kernel(
             w2_scale[:].bitcast(I32).rearrange("p (a t b w) -> p a t b w", a=PASSES, t=PACK, w=2),
             w2_scale_raw[:].bitcast(I32).rearrange("p (a b t w) -> p a t b w", a=PASSES, t=PACK, w=2),
         )
-        gather_words(1, 0, PIECE)
-        gather_words(1, PIECE, S)
+        gather_words(1, 0, QUARTER)
+        gather_words(1, QUARTER, 2 * QUARTER)
+        gather_words(1, 2 * QUARTER, S)
 
         w1_raw = [held([P, PACK, H], F32, "w1_raw%d" % a, (22400, 0)[a]) for a in range(PASSES)]
         w3_raw = held([P, PASSES * H], I32, "w3_raw", 16384)
         w3_scale_raw = held([P, H], U8, "w3_scale_raw", 20480)
         w6_scale = held([P, N], U8, "w6_scale", 34688)
         w6_codes = held([P, 2 * N], U8, "w6_codes", 34944)
-        gains["h3"] = held([P, PACK], F32, "gain_h3", 21760)
         w5_raw = held([P, PACK, N], F32, "w5_raw", 30592)
         w4_raw = held([P, PACK, N], F32, "w4_raw", 35584)
         for plane in (w3_scale_raw, w6_scale):
@@ -143,10 +132,15 @@ def tile_list_land_air_exchange_kernel(
                 w3_scale_raw[32 * d : 32 * d + 4 * PASSES, :].bitcast(I32),
                 w3_scales[:, 4 * d : 4 * d + 4, :].bitcast(I32),
             )
+        gain3_columns = held([P, PACK], F32, "gain3_columns", 21760)
+        nc.sync.dma_start(gain3_columns[:], gain3.rearrange("(p t) -> p t", t=PACK))
         for a in range(PASSES):
             nc.sync.dma_start(w1_raw[a][:], w1_rows[a])
-        nc.sync.dma_start(gains["h3"][:], gain3.rearrange("(p t) -> p t", t=PACK))
-        gain1_raw = load_gain_columns(nc.sync, gain1, 4, "gain1_raw", 35456)
+        nc.sync.dma_start(gain_rows[0:1, :], gain3.unsqueeze(0))
+        nc.sync.dma_start(
+            gain_rows[1 : 1 + PACK, 0:P].rearrange("t (e i) -> t e i", i=4),
+            gain1.rearrange("(e t i) -> t e i", t=PACK, i=4),
+        )
         for t in range(PACK):
             nc.sync.dma_start(w5_raw[:, t, :], w5.rearrange("(b t i) n -> t b i n", t=PACK, i=8)[t])
         for t in range(PACK):
@@ -157,8 +151,24 @@ def tile_list_land_air_exchange_kernel(
                 w6_scale[32 * d : 32 * d + 4, :].bitcast(I32), w6_scales[0, 4 * d : 4 * d + 4, :].bitcast(I32)
             )
 
-        w3_codes = held([P, PASSES * H], I32, "w3_codes", 39680)
-        w3_scale = held([P, H], U8, "w3_scale", 43776)
+        gain_bank = gain_banks.tile([P, PACK * GAIN_STEP + P], F32, name="gain_bank")
+        gains["h1"] = gain_bank[:, 1 : 1 + PACK]
+        gains["h3"] = gain3_columns
+        gain_columns = {"h3": gain3_columns}
+
+        def turn_gains():
+            gains["h3"] = gain_bank[:, GAIN_STEP : GAIN_STEP * (PACK + 1) : GAIN_STEP]
+            nc.tensor.transpose(gain_bank[:, 0:P], gain_rows[:, 0:P], identity[:])
+            for t in range(PACK):
+                c0 = GAIN_STEP * (t + 1)
+                nc.tensor.transpose(gain_bank[:, c0 : c0 + P], gain_rows[:, t:H:PACK], identity[:])
+
+        def copy_gains(name):
+            gain_columns[name] = held([P, PACK], F32, "gain_columns_" + name)
+            nc.scalar.copy(gain_columns[name][:], gains[name])
+
+        w3_codes = held([P, PASSES * H], I32, "w3_codes")
+        w3_scale = held([P, H], U8, "w3_scale")
 
         def order_w3():
             nc.vector.tensor_copy(
@@ -175,10 +185,10 @@ def tile_list_land_air_exchange_kernel(
         w1_codes = held([P, PASSES * H], U32, "w1_codes")
         w1_scale = held([P, PASSES * H], U8, "w1_scale")
 
-        def round_w1(a, t):
-            nc.scalar.copy(
-                w1_round[a][:, t].rearrange("p (e i) j -> p e j i", i=4),
-                w1_raw[a][:].rearrange("p j (e t i) -> p t e j i", t=PACK, i=4)[:, t],
+        def round_w1(copy, a, t0, t1):
+            copy(
+                w1_round[a][:, t0:t1].rearrange("p t (e i) j -> p t e j i", i=4),
+                w1_raw[a][:].rearrange("p j (e t i) -> p t e j i", t=PACK, i=4)[:, t0:t1],
             )
 
         def quantize_w1(a):
@@ -217,140 +227,205 @@ def tile_list_land_air_exchange_kernel(
             codes, scale = second["w4" if name == "h1" else "w5"]
             return codes[:, u * P : (u + 1) * P].bitcast(E4M3), scale[:, u * P : (u + 1) * P]
 
-        h_codes = {name: held([P, S], U32, name + "_codes") for name in ("h1", "h2", "h3")}
-        h_scale = {name: held([P, S], U8, name + "_scale") for name in ("h1", "h2", "h3")}
-        rounded_h = {}
+        names = ("h1", "h2", "h3")
+        h_codes = {name: held([P, S], U32, name + "_codes") for name in names}
+        h_scale = {name: held([P, S], U8, name + "_scale") for name in names}
+        tanhs = {name: held([P, S * PACK], F32, name + "_tanh") for name in ("h2", "h3")}
+        pairs = {name: held([P, S * PACK], F32, name + "_pairs") for name in ("h1", "h3")}
+        paired = set()
+        stage = held([P, 4 * S * PACK], BF16, "stage")
+        stage_ends = [0, 2 * S * PACK]
+        placed = {}
 
-        banks = {}
-        tanhs = {}
+        def by_slot(run):
+            return run.rearrange("p (j t) -> p j t", t=PACK)
 
-        def first_pass(name, chunk, a):
-            if a == 0:
-                banks[name, chunk] = psum.tile([P, PACK, CHUNK], F32, name="first_bank")
+        def tanh_chunk(name, chunk):
+            bank = first_banks.tile([P, PACK, CHUNK], F32, name="first_bank")
             j0 = chunk * CHUNK
-            for t in range(PACK):
-                codes, scale = first_weight(name, a, t)
-                nc.tensor.matmul_mx(
-                    banks[name, chunk][:, t, :],
-                    lhsT=codes,
-                    lhsT_scale=scale,
-                    rhs=v_codes[a][:, j0 : j0 + CHUNK].bitcast(E4M3),
-                    rhs_scale=v_scale[:, a * S + j0 : a * S + j0 + CHUNK],
-                    start=(a == 0 and t == 0),
-                    stop=(a == PASSES - 1 and t == PACK - 1),
-                )
-
-        def activate(name, chunk, piece):
-            start, width = piece
-            c0 = chunk * CHUNK - start
-            if c0 == 0:
-                if (name, chunk) == ("h2", 1):
-                    tanhs[name, piece] = held([P, width, PACK], F32, "tanh_early", 39680)
-                else:
-                    tanhs[name, piece] = ring.tile([P, width, PACK], F32, name="tanh")
+            for a in range(PASSES):
+                for t in range(PACK):
+                    codes, scale = first_weight(name, a, t)
+                    nc.tensor.matmul_mx(
+                        bank[:, t, :],
+                        lhsT=codes,
+                        lhsT_scale=scale,
+                        rhs=v_codes[a][:, j0 : j0 + CHUNK].bitcast(E4M3),
+                        rhs_scale=v_scale[:, a * S + j0 : a * S + j0 + CHUNK],
+                        start=(a == 0 and t == 0),
+                        stop=(a == PASSES - 1 and t == PACK - 1),
+                    )
             nc.scalar.activation(
-                tanhs[name, piece][:, c0 : c0 + CHUNK, :], banks[name, chunk][:].rearrange("p t j -> p j t"), TANH
+                by_slot(tanhs[name][:, PACK * j0 : PACK * (j0 + CHUNK)]), bank[:].rearrange("p t j -> p j t"), TANH
             )
 
-        def apply_gain(name, piece):
-            width = piece[1]
-            if (name, piece) == ("h2", (CHUNK, CHUNK)):
-                rounded = held([P, width, PACK], BF16, "rounded_early", 43776)
-            else:
-                rounded = ring.tile([P, width, PACK], BF16, name="rounded", align_bytes=64)
-            nc.vector.tensor_tensor(
-                rounded[:], tanhs[name, piece][:], gains[name][:].unsqueeze(1).to_broadcast([P, width, PACK]), MULT
+        def tanh_pair(name, quarter, u):
+            bank = first_banks.tile([P, 2, QUARTER], F32, name="first_bank")
+            j0 = quarter * QUARTER
+            paired.add((name, j0))
+            for a in range(PASSES):
+                for e in range(2):
+                    codes, scale = first_weight(name, a, 2 * u + e)
+                    nc.tensor.matmul_mx(
+                        bank[:, e, :],
+                        lhsT=codes,
+                        lhsT_scale=scale,
+                        rhs=v_codes[a][:, j0 : j0 + QUARTER].bitcast(E4M3),
+                        rhs_scale=v_scale[:, a * S + j0 : a * S + j0 + QUARTER],
+                        start=(a == 0 and e == 0),
+                        stop=(a == PASSES - 1 and e == 1),
+                    )
+            c0 = 2 * (u * S + j0)
+            nc.scalar.activation(
+                pairs[name][:, c0 : c0 + 2 * QUARTER].rearrange("p (j e) -> p j e", e=2),
+                bank[:].rearrange("p e j -> p j e"),
+                TANH,
             )
-            rounded_h[name, piece] = rounded
 
-        def quantize_h(name, piece):
-            cols = slice(piece[0], piece[0] + piece[1])
+        def tanh_columns(name, start, c0, c1):
+            if (name, start) in paired:
+                return pairs[name][:].rearrange("p (u j e) -> p j u e", u=2, e=2)[:, start + c0 : start + c1]
+            return tanhs[name][:, PACK * (start + c0) : PACK * (start + c1)].rearrange("p (j u e) -> p j u e", u=2, e=2)
+
+        def apply_gain(name, start, width, share=0):
+            lane = len(placed) % 2
+            at = stage_ends[lane] - PACK * share
+            stage_ends[lane] = at + PACK * width
+            placed[name, start] = (at, width)
+            for engine, gain, c0, c1 in (
+                (nc.gpsimd, gain_columns.get(name), 0, share),
+                (nc.vector, gains[name], share, width),
+            ):
+                if c1 > c0:
+                    engine.tensor_tensor(
+                        stage[:, at + PACK * c0 : at + PACK * c1].rearrange("p (j u e) -> p j u e", u=2, e=2),
+                        tanh_columns(name, start, c0, c1),
+                        gain[:].rearrange("p (u e) -> p u e", e=2).unsqueeze(1).to_broadcast([P, c1 - c0, 2, 2]),
+                        MULT,
+                    )
+
+        def quantize_h(name, start):
+            at, width = placed[name, start]
             nc.vector.quantize_mx(
-                h_codes[name][:, cols].bitcast(E4M3),
-                h_scale[name][:, cols],
-                rounded_h[name, piece][:].rearrange("p j t -> p (j t)"),
+                h_codes[name][:, start : start + width].bitcast(E4M3),
+                h_scale[name][:, start : start + width],
+                stage[:, at : at + PACK * width],
             )
 
-        def second_stage(name, piece):
-            cols = slice(piece[0], piece[0] + piece[1])
-            bank = psum.tile([P, HALVES, piece[1]], F32, name="second_bank")
+        def second_stage(name, start, width):
+            bank = second_banks.tile([P, HALVES, width], F32, name="second_bank")
             for u in range(HALVES):
                 codes, scale = second_weight(name, u)
                 nc.tensor.matmul_mx(
                     bank[:, u, :],
                     lhsT=codes,
                     lhsT_scale=scale,
-                    rhs=h_codes[name][:, cols].bitcast(E4M3),
-                    rhs_scale=h_scale[name][:, cols],
+                    rhs=h_codes[name][:, start : start + width].bitcast(E4M3),
+                    rhs_scale=h_scale[name][:, start : start + width],
                     start=True,
                     stop=True,
                 )
             return bank
 
         y2 = held([P, HALVES, S], F32, "y2")
+        product = held([P, HALVES, S], F32, "product")
 
-        def park_y2(piece):
-            nc.scalar.copy(y2[:, :, piece[0] : piece[0] + piece[1]], second_stage("h2", piece)[:])
+        def park_y2(start, width):
+            nc.scalar.copy(y2[:, :, start : start + width], second_stage("h2", start, width)[:])
 
-        products = {}
-
-        def multiply(piece):
-            product = ring.tile([P, HALVES, piece[1]], F32, name="product")
+        def multiply(start, width):
             nc.vector.tensor_tensor(
-                product[:], second_stage("h1", piece)[:], y2[:, :, piece[0] : piece[0] + piece[1]], MULT
-            )
-            products[piece] = product
-
-        def finish(piece):
-            result = ring.tile([P, HALVES, piece[1]], F32, name="result")
-            nc.vector.tensor_tensor(result[:], second_stage("h3", piece)[:], products[piece][:], ADD)
-            nc.sync.dma_start(
-                out.rearrange("(u p) j -> p u j", p=P)[:, :, piece[0] : piece[0] + piece[1]], result[:]
+                product[:, :, start : start + width],
+                second_stage("h1", start, width)[:],
+                y2[:, :, start : start + width],
+                MULT,
             )
 
-        def cut(widths):
-            return [(sum(widths[:i]), w) for i, w in enumerate(widths)]
+        def finish(start, width):
+            result = ring.tile([P, HALVES, width], F32, name="result")
+            nc.vector.tensor_tensor(
+                result[:], second_stage("h3", start, width)[:], product[:, :, start : start + width], ADD
+            )
+            nc.sync.dma_start(out.rearrange("(u p) j -> p u j", p=P)[:, :, start : start + width], result[:])
 
-        pieces = {"h2": cut([128, 128, 256, 512]), "h3": cut([512, 512]), "h1": cut([256, 256, 256, 128, 128])}
-        quarters = cut([PIECE] * PIECES)
-        last = pieces["h1"]
-        chunks = S // CHUNK
-        after = {
-            ("h2", 1): [order_w3],
-            ("h2", 3): [order_w3_scale],
-            ("h2", 7): [lambda: quantize_w1(0)],
-            ("h3", 4): [lambda: quantize_w1(1), lambda: pack_gain("h1", gain1_raw)],
-            ("h1", 0): [lambda: round_second("w5", w5_raw)],
-            ("h1", 1): [lambda: quantize_second("w5"), lambda: round_second("w4", w4_raw)],
-            ("h1", 2): [lambda: park_y2(quarters[0]), lambda: quantize_second("w4")],
-            ("h1", 3): [lambda: park_y2(quarters[1]), lambda: multiply(last[0])],
-            ("h1", 5): [lambda: park_y2(quarters[2]), lambda: finish(last[0]), lambda: multiply(last[1])],
-            ("h1", 6): [lambda: park_y2(quarters[3]), lambda: finish(last[1]), lambda: multiply(last[2])],
-            ("h1", 7): [lambda: finish(last[2]), lambda: multiply(last[3])],
-        }
-        rounding = [(a, t) for a in range(PASSES) for t in range(PACK)]
-        waiting = []
-        for chunk in range(2):
-            first_pass("h2", chunk, 0)
-        step = 0
-        for name in ("h2", "h3", "h1"):
-            for piece in pieces[name]:
-                for chunk in range(piece[0] // CHUNK, (piece[0] + piece[1]) // CHUNK):
-                    if step >= 2:
-                        first_pass(name, chunk, 0)
-                    first_pass(name, chunk, 1)
-                    activate(name, chunk, piece)
-                    if 3 <= step < 3 + len(rounding):
-                        round_w1(*rounding[step - 3])
-                    if (chunk + 1) * CHUNK == piece[0] + piece[1]:
-                        apply_gain(name, piece)
-                        for earlier in waiting:
-                            quantize_h(*earlier)
-                        waiting = [(name, piece)]
-                    for call in after.get((name, chunk), []):
-                        call()
-                    step = step + 1
-        quantize_h("h1", last[4])
-        finish(last[3])
-        multiply(last[4])
-        finish(last[4])
+        tanh_chunk("h2", 0)
+        apply_gain("h2", 0, 128)
+        tanh_chunk("h2", 1)
+        apply_gain("h2", 128, 128)
+        quantize_h("h2", 0)
+        tanh_chunk("h2", 2)
+        tanh_chunk("h2", 3)
+        order_w3()
+        order_w3_scale()
+        apply_gain("h2", 256, 256)
+        quantize_h("h2", 128)
+        tanh_chunk("h2", 4)
+        tanh_chunk("h2", 5)
+        round_w1(nc.scalar.copy, 0, 0, 1)
+        apply_gain("h2", 512, 256)
+        quantize_h("h2", 256)
+        tanh_chunk("h2", 6)
+        round_w1(nc.scalar.copy, 0, 1, 2)
+        tanh_chunk("h2", 7)
+        round_w1(nc.scalar.copy, 0, 2, 3)
+        round_w1(nc.vector.tensor_copy, 1, 2, 4)
+        apply_gain("h2", 768, 256)
+        quantize_h("h2", 512)
+        tanh_pair("h3", 0, 0)
+        round_w1(nc.scalar.copy, 0, 3, 4)
+        tanh_pair("h3", 0, 1)
+        round_w1(nc.scalar.copy, 1, 0, 1)
+        quantize_w1(0)
+        apply_gain("h3", 0, 256)
+        quantize_h("h2", 768)
+        tanh_pair("h3", 1, 0)
+        round_w1(nc.scalar.copy, 1, 1, 2)
+        quantize_w1(1)
+        tanh_pair("h3", 1, 1)
+        turn_gains()
+        apply_gain("h3", 256, 256)
+        quantize_h("h3", 0)
+        tanh_pair("h3", 2, 0)
+        tanh_pair("h3", 2, 1)
+        round_second("w5", w5_raw)
+        apply_gain("h3", 512, 256, 0)
+        quantize_h("h3", 256)
+        tanh_pair("h1", 0, 0)
+        tanh_pair("h1", 0, 1)
+        quantize_second("w5")
+        round_second("w4", w4_raw)
+        apply_gain("h1", 0, 256, 0)
+        quantize_h("h3", 512)
+        tanh_pair("h1", 1, 0)
+        tanh_pair("h1", 1, 1)
+        quantize_second("w4")
+        park_y2(0, 256)
+        apply_gain("h1", 256, 256, 0)
+        quantize_h("h1", 0)
+        tanh_pair("h1", 2, 0)
+        tanh_pair("h1", 2, 1)
+        park_y2(256, 256)
+        apply_gain("h1", 512, 256, 0)
+        multiply(0, 256)
+        quantize_h("h1", 256)
+        tanh_pair("h1", 3, 0)
+        tanh_pair("h1", 3, 1)
+        park_y2(512, 256)
+        finish(0, 256)
+        apply_gain("h1", 768, 256, 0)
+        multiply(256, 256)
+        quantize_h("h1", 512)
+        tanh_chunk("h3", 6)
+        tanh_chunk("h3", 7)
+        park_y2(768, 256)
+        finish(256, 256)
+        apply_gain("h3", 768, 128, 0)
+        multiply(512, 256)
+        quantize_h("h1", 768)
+        finish(512, 256)
+        apply_gain("h3", 896, 128, 0)
+        quantize_h("h3", 768)
+        multiply(768, 256)
+        quantize_h("h3", 896)
+        finish(768, 128)
+        finish(896, 128)

@@ -383,6 +383,7 @@ def tile_list_land_air_exchange_kernel(
         quantize_w1(1)
         tanh_pair("h3", 1, 1)
         turn_gains()
+        copy_gains("h1")
         apply_gain("h3", 256, 256)
         quantize_h("h3", 0)
         tanh_pair("h3", 2, 0)
@@ -394,36 +395,36 @@ def tile_list_land_air_exchange_kernel(
         tanh_pair("h1", 0, 1)
         quantize_second("w5")
         round_second("w4", w4_raw)
-        apply_gain("h1", 0, 256, 0)
+        apply_gain("h1", 0, 256, 64)
         quantize_h("h3", 512)
         tanh_pair("h1", 1, 0)
         tanh_pair("h1", 1, 1)
         quantize_second("w4")
         park_y2(0, 256)
-        apply_gain("h1", 256, 256, 0)
+        apply_gain("h1", 256, 256, 64)
         quantize_h("h1", 0)
         tanh_pair("h1", 2, 0)
         tanh_pair("h1", 2, 1)
         park_y2(256, 256)
-        apply_gain("h1", 512, 256, 0)
+        apply_gain("h1", 512, 256, 96)
         multiply(0, 256)
         quantize_h("h1", 256)
         tanh_pair("h1", 3, 0)
         tanh_pair("h1", 3, 1)
         park_y2(512, 256)
         finish(0, 256)
-        apply_gain("h1", 768, 256, 0)
+        apply_gain("h1", 768, 256, 96)
         multiply(256, 256)
         quantize_h("h1", 512)
         tanh_chunk("h3", 6)
         tanh_chunk("h3", 7)
         park_y2(768, 256)
         finish(256, 256)
-        apply_gain("h3", 768, 128, 0)
+        apply_gain("h3", 768, 128, 48)
         multiply(512, 256)
         quantize_h("h1", 768)
         finish(512, 256)
-        apply_gain("h3", 896, 128, 0)
+        apply_gain("h3", 896, 128, 48)
         quantize_h("h3", 768)
         multiply(768, 256)
         quantize_h("h3", 896)

@@ -368,18 +368,16 @@ def tile_list_land_air_exchange_kernel(
         round_w1(nc.scalar.copy, 0, 1, 2)
         tanh_chunk("h2", 7)
         round_w1(nc.scalar.copy, 0, 2, 3)
-        round_w1(nc.vector.tensor_copy, 1, 2, 4)
+        round_w1(nc.vector.tensor_copy, 1, 0, 4)
         apply_gain("h2", 768, 256)
         quantize_h("h2", 512)
         tanh_pair("h3", 0, 0)
         round_w1(nc.scalar.copy, 0, 3, 4)
         tanh_pair("h3", 0, 1)
-        round_w1(nc.scalar.copy, 1, 0, 1)
         quantize_w1(0)
         apply_gain("h3", 0, 256)
         quantize_h("h2", 768)
         tanh_pair("h3", 1, 0)
-        round_w1(nc.scalar.copy, 1, 1, 2)
         quantize_w1(1)
         tanh_pair("h3", 1, 1)
         turn_gains()
@@ -389,7 +387,7 @@ def tile_list_land_air_exchange_kernel(
         tanh_pair("h3", 2, 0)
         tanh_pair("h3", 2, 1)
         round_second("w5", w5_raw)
-        apply_gain("h3", 512, 256, 0)
+        apply_gain("h3", 512, 256, 56)
         quantize_h("h3", 256)
         tanh_pair("h1", 0, 0)
         tanh_pair("h1", 0, 1)
@@ -406,25 +404,25 @@ def tile_list_land_air_exchange_kernel(
         tanh_pair("h1", 2, 0)
         tanh_pair("h1", 2, 1)
         park_y2(256, 256)
-        apply_gain("h1", 512, 256, 96)
+        apply_gain("h1", 512, 256, 112)
         multiply(0, 256)
         quantize_h("h1", 256)
         tanh_pair("h1", 3, 0)
         tanh_pair("h1", 3, 1)
         park_y2(512, 256)
         finish(0, 256)
-        apply_gain("h1", 768, 256, 96)
+        apply_gain("h1", 768, 256, 112)
         multiply(256, 256)
         quantize_h("h1", 512)
         tanh_chunk("h3", 6)
         tanh_chunk("h3", 7)
         park_y2(768, 256)
         finish(256, 256)
-        apply_gain("h3", 768, 128, 48)
+        apply_gain("h3", 768, 128, 64)
         multiply(512, 256)
         quantize_h("h1", 768)
         finish(512, 256)
-        apply_gain("h3", 896, 128, 48)
+        apply_gain("h3", 896, 128, 64)
         quantize_h("h3", 768)
         multiply(768, 256)
         quantize_h("h3", 896)

@@ -387,7 +387,7 @@ def tile_list_land_air_exchange_kernel(
         tanh_pair("h3", 2, 0)
         tanh_pair("h3", 2, 1)
         round_second("w5", w5_raw)
-        apply_gain("h3", 512, 256, 56)
+        apply_gain("h3", 512, 256, 0)
         quantize_h("h3", 256)
         tanh_pair("h1", 0, 0)
         tanh_pair("h1", 0, 1)
@@ -404,25 +404,25 @@ def tile_list_land_air_exchange_kernel(
         tanh_pair("h1", 2, 0)
         tanh_pair("h1", 2, 1)
         park_y2(256, 256)
-        apply_gain("h1", 512, 256, 112)
+        apply_gain("h1", 512, 256, 96)
         multiply(0, 256)
         quantize_h("h1", 256)
         tanh_pair("h1", 3, 0)
         tanh_pair("h1", 3, 1)
         park_y2(512, 256)
         finish(0, 256)
-        apply_gain("h1", 768, 256, 112)
+        apply_gain("h1", 768, 256, 96)
         multiply(256, 256)
         quantize_h("h1", 512)
         tanh_chunk("h3", 6)
         tanh_chunk("h3", 7)
         park_y2(768, 256)
         finish(256, 256)
-        apply_gain("h3", 768, 128, 64)
+        apply_gain("h3", 768, 128, 48)
         multiply(512, 256)
         quantize_h("h1", 768)
         finish(512, 256)
-        apply_gain("h3", 896, 128, 64)
+        apply_gain("h3", 896, 128, 48)
         quantize_h("h3", 768)
         multiply(768, 256)
         quantize_h("h3", 896)

@@ -24,7 +24,6 @@ PASSES = K // (P * PACK)
 CHUNK = 128
 QUARTER = 256
 HALVES = N // P
-GAIN_STEP = 16
 
 
 def tile_list_land_air_exchange_kernel(
@@ -57,14 +56,16 @@ def tile_list_land_air_exchange_kernel(
         word_window = [held([P, T], U32, "word_window%d" % a, 8192 * a) for a in range(PASSES)]
         w2_raw = held([P, PASSES * H * 2], U8, "w2_raw", 20416)
         w2_scale_raw = held([P, PASSES * H], U8, "w2_scale_raw")
+        w3_scale_raw = held([P, H], U8, "w3_scale_raw")
+        w6_scale = held([P, N], U8, "w6_scale")
         gain2_rows = held([P, P], F32, "gain2_rows")
         gain_rows = held([P, H], F32, "gain_rows")
         identity = held([P, P], F32, "identity")
         v_scale = held([P, PASSES * S], U8, "v_scale")
         nc.gpsimd.memset(w2_scale_raw[:].bitcast(I32), 0)
         nc.gpsimd.memset(gain2_rows[:], 0.0)
+        nc.gpsimd.memset(w3_scale_raw[:].bitcast(I32), 0)
         make_identity(nc, identity[:])
-        nc.gpsimd.memset(gain_rows[:], 0.0)
         nc.vector.memset(v_scale[:, S:].bitcast(I32), 0)
         nc.sync.dma_start(
             w2_raw[:].bitcast(I32).rearrange("p (a c) -> p a c", a=PASSES),
@@ -80,10 +81,31 @@ def tile_list_land_air_exchange_kernel(
             gain2_rows[0:PACK, :].rearrange("t (b i) -> t b i", i=8), gain2.rearrange("(b t i) -> t b i", t=PACK, i=8)
         )
         nc.sync.dma_start(word_window[1][:].bitcast(I32), tab_words[1].rearrange("p t i -> p (t i)").bitcast(I32))
+        for d in range(4):
+            nc.gpsimd.dma_start(
+                w3_scale_raw[32 * d : 32 * d + 4 * PASSES, :].bitcast(I32),
+                w3_scales[:, 4 * d : 4 * d + 4, :].bitcast(I32),
+            )
 
+        nc.gpsimd.memset(gain_rows[:], 0.0)
+        nc.gpsimd.memset(w6_scale[:].bitcast(I32), 0)
         gain2_bank = second_banks.tile([P, P], F32, name="second_bank")
         nc.tensor.transpose(gain2_bank[:], gain2_rows[:], identity[:])
-        gains = {"h2": gain2_bank[:, 0:PACK]}
+        gain_bank = gain_banks.tile([P, PACK + P], F32, name="gain_bank")
+        gain_at = {"h3": 0, "h1": 8}
+        gains = {name: gain_bank[:, at : at + PACK] for name, at in gain_at.items()}
+        gains["h2"] = gain2_bank[:, 0:PACK]
+        gain_copy = held([P, 12], F32, "gain_copy", 16384)
+        gain_columns = {name: gain_copy[:, at : at + PACK] for name, at in gain_at.items()}
+        gain2_copy = held([P, PACK], F32, "gain2_copy")
+        nc.vector.tensor_copy(gain2_copy[:], gains["h2"])
+        gain_columns["h2"] = gain2_copy[:]
+
+        def copy_gains():
+            for t in range(PACK):
+                nc.tensor.transpose(gain_bank[:, t : t + P], gain_rows[:, t:H:PACK], identity[:])
+            nc.tensor.transpose(gain_bank[:, PACK : PACK + P], gain_rows[:, 0:P], identity[:])
+            nc.scalar.copy(gain_copy[:], gain_bank[:, 0:12])
 
         picked_scale = held([P, S], U8, "picked_scale", 34624)
         nc.vector.tensor_copy(picked_scale[:], scale_window[:].indirect(offsets[:]))
@@ -115,31 +137,19 @@ def tile_list_land_air_exchange_kernel(
 
         w1_raw = [held([P, PACK, H], F32, "w1_raw%d" % a, (22400, 0)[a]) for a in range(PASSES)]
         w3_raw = held([P, PASSES * H], I32, "w3_raw", 16384)
-        w3_scale_raw = held([P, H], U8, "w3_scale_raw", 20480)
-        w6_scale = held([P, N], U8, "w6_scale", 34688)
         w6_codes = held([P, 2 * N], U8, "w6_codes", 34944)
         w5_raw = held([P, PACK, N], F32, "w5_raw", 30592)
         w4_raw = held([P, PACK, N], F32, "w4_raw", 35584)
-        for plane in (w3_scale_raw, w6_scale):
-            nc.gpsimd.memset(plane[:].bitcast(I32), 0)
         w1_rows = w1.rearrange("(a p j) r -> a p j r", a=PASSES, j=PACK)
         nc.sync.dma_start(
             w3_raw[:].rearrange("p (a c) -> p a c", a=PASSES),
             w3_words.rearrange("a p c i -> p a (c i)").bitcast(I32),
         )
-        for d in range(4):
-            nc.sync.dma_start(
-                w3_scale_raw[32 * d : 32 * d + 4 * PASSES, :].bitcast(I32),
-                w3_scales[:, 4 * d : 4 * d + 4, :].bitcast(I32),
-            )
-        gain3_columns = held([P, PACK], F32, "gain3_columns", 21760)
-        nc.sync.dma_start(gain3_columns[:], gain3.rearrange("(p t) -> p t", t=PACK))
         for a in range(PASSES):
             nc.sync.dma_start(w1_raw[a][:], w1_rows[a])
         nc.sync.dma_start(gain_rows[0:1, :], gain3.unsqueeze(0))
         nc.sync.dma_start(
-            gain_rows[1 : 1 + PACK, 0:P].rearrange("t (e i) -> t e i", i=4),
-            gain1.rearrange("(e t i) -> t e i", t=PACK, i=4),
+            gain_rows[4:8, 0:P].rearrange("t (e i) -> t e i", i=4), gain1.rearrange("(e t i) -> t e i", t=PACK, i=4)
         )
         for t in range(PACK):
             nc.sync.dma_start(w5_raw[:, t, :], w5.rearrange("(b t i) n -> t b i n", t=PACK, i=8)[t])
@@ -151,24 +161,8 @@ def tile_list_land_air_exchange_kernel(
                 w6_scale[32 * d : 32 * d + 4, :].bitcast(I32), w6_scales[0, 4 * d : 4 * d + 4, :].bitcast(I32)
             )
 
-        gain_bank = gain_banks.tile([P, PACK * GAIN_STEP + P], F32, name="gain_bank")
-        gains["h1"] = gain_bank[:, 1 : 1 + PACK]
-        gains["h3"] = gain3_columns
-        gain_columns = {"h3": gain3_columns}
-
-        def turn_gains():
-            gains["h3"] = gain_bank[:, GAIN_STEP : GAIN_STEP * (PACK + 1) : GAIN_STEP]
-            nc.tensor.transpose(gain_bank[:, 0:P], gain_rows[:, 0:P], identity[:])
-            for t in range(PACK):
-                c0 = GAIN_STEP * (t + 1)
-                nc.tensor.transpose(gain_bank[:, c0 : c0 + P], gain_rows[:, t:H:PACK], identity[:])
-
-        def copy_gains(name):
-            gain_columns[name] = held([P, PACK], F32, "gain_columns_" + name)
-            nc.scalar.copy(gain_columns[name][:], gains[name])
-
         w3_codes = held([P, PASSES * H], I32, "w3_codes")
-        w3_scale = held([P, H], U8, "w3_scale")
+        w3_scale = held([P, H], U8, "w3_scale", 16448)
 
         def order_w3():
             nc.vector.tensor_copy(
@@ -200,9 +194,9 @@ def tile_list_land_air_exchange_kernel(
 
         second = {}
 
-        def round_second(name, raw):
+        def round_second(copy, name, raw):
             rounded = held([P, N, PACK], BF16, name + "_round")
-            nc.scalar.copy(
+            copy(
                 rounded[:].rearrange("p (c i) t -> p c t i", i=4), raw[:].rearrange("p t (c i) -> p c t i", i=4)
             )
             second[name] = rounded
@@ -233,8 +227,8 @@ def tile_list_land_air_exchange_kernel(
         tanhs = {name: held([P, S * PACK], F32, name + "_tanh") for name in ("h2", "h3")}
         pairs = {name: held([P, S * PACK], F32, name + "_pairs") for name in ("h1", "h3")}
         paired = set()
-        stage = held([P, 4 * S * PACK], BF16, "stage")
-        stage_ends = [0, 2 * S * PACK]
+        stage = held([P, 3 * S * PACK], BF16, "stage")
+        stage_end = [0]
         placed = {}
 
         def by_slot(run):
@@ -287,25 +281,28 @@ def tile_list_land_air_exchange_kernel(
                 return pairs[name][:].rearrange("p (u j e) -> p j u e", u=2, e=2)[:, start + c0 : start + c1]
             return tanhs[name][:, PACK * (start + c0) : PACK * (start + c1)].rearrange("p (j u e) -> p j u e", u=2, e=2)
 
-        def apply_gain(name, start, width, share=0):
-            lane = len(placed) % 2
-            at = stage_ends[lane] - PACK * share
-            stage_ends[lane] = at + PACK * width
-            placed[name, start] = (at, width)
-            for engine, gain, c0, c1 in (
-                (nc.gpsimd, gain_columns.get(name), 0, share),
-                (nc.vector, gains[name], share, width),
-            ):
-                if c1 > c0:
-                    engine.tensor_tensor(
-                        stage[:, at + PACK * c0 : at + PACK * c1].rearrange("p (j u e) -> p j u e", u=2, e=2),
-                        tanh_columns(name, start, c0, c1),
-                        gain[:].rearrange("p (u e) -> p u e", e=2).unsqueeze(1).to_broadcast([P, c1 - c0, 2, 2]),
-                        MULT,
-                    )
+        def place(name, start, width, share=0):
+            at = stage_end[0] - PACK * share
+            stage_end[0] = at + PACK * width
+            placed[name, start] = at
+            if share:
+                apply_gain(nc.gpsimd, gain_columns[name], name, start, 0, share)
 
-        def quantize_h(name, start):
-            at, width = placed[name, start]
+        def apply_gain(engine, gain, name, start, c0, c1):
+            at = placed[name, start]
+            engine.tensor_tensor(
+                stage[:, at + PACK * c0 : at + PACK * c1].rearrange("p (j u e) -> p j u e", u=2, e=2),
+                tanh_columns(name, start, c0, c1),
+                gain.rearrange("p (u e) -> p u e", e=2).unsqueeze(1).to_broadcast([P, c1 - c0, 2, 2]),
+                MULT,
+            )
+
+        def gain_piece(name, start, width, share=0):
+            place(name, start, width, share)
+            apply_gain(nc.vector, gains[name], name, start, share, width)
+
+        def quantize_h(name, start, width):
+            at = placed[name, start]
             nc.vector.quantize_mx(
                 h_codes[name][:, start : start + width].bitcast(E4M3),
                 h_scale[name][:, start : start + width],
@@ -349,82 +346,78 @@ def tile_list_land_air_exchange_kernel(
             nc.sync.dma_start(out.rearrange("(u p) j -> p u j", p=P)[:, :, start : start + width], result[:])
 
         tanh_chunk("h2", 0)
-        apply_gain("h2", 0, 128)
+        place("h2", 0, 256)
+        apply_gain(nc.vector, gains["h2"], "h2", 0, 0, 128)
         tanh_chunk("h2", 1)
-        apply_gain("h2", 128, 128)
-        quantize_h("h2", 0)
-        tanh_chunk("h2", 2)
-        tanh_chunk("h2", 3)
+        apply_gain(nc.vector, gains["h2"], "h2", 0, 128, 256)
         order_w3()
         order_w3_scale()
-        apply_gain("h2", 256, 256)
-        quantize_h("h2", 128)
+        quantize_h("h2", 0, 256)
+        tanh_chunk("h2", 2)
+        tanh_chunk("h2", 3)
+        place("h2", 256, 512, 128)
+        apply_gain(nc.vector, gains["h2"], "h2", 256, 128, 256)
         tanh_chunk("h2", 4)
         tanh_chunk("h2", 5)
+        apply_gain(nc.vector, gains["h2"], "h2", 256, 256, 512)
         round_w1(nc.scalar.copy, 0, 0, 1)
-        apply_gain("h2", 512, 256)
-        quantize_h("h2", 256)
         tanh_chunk("h2", 6)
         round_w1(nc.scalar.copy, 0, 1, 2)
         tanh_chunk("h2", 7)
         round_w1(nc.scalar.copy, 0, 2, 3)
         round_w1(nc.vector.tensor_copy, 1, 0, 4)
-        apply_gain("h2", 768, 256)
-        quantize_h("h2", 512)
-        tanh_pair("h3", 0, 0)
+        quantize_h("h2", 256, 512)
+        gain_piece("h2", 768, 256, 40)
         round_w1(nc.scalar.copy, 0, 3, 4)
-        tanh_pair("h3", 0, 1)
-        quantize_w1(0)
-        apply_gain("h3", 0, 256)
-        quantize_h("h2", 768)
-        tanh_pair("h3", 1, 0)
         quantize_w1(1)
+        quantize_w1(0)
+        quantize_h("h2", 768, 256)
+        tanh_pair("h3", 0, 0)
+        tanh_pair("h3", 0, 1)
+        copy_gains()
+        tanh_pair("h3", 1, 0)
         tanh_pair("h3", 1, 1)
-        turn_gains()
-        copy_gains("h1")
-        apply_gain("h3", 256, 256)
-        quantize_h("h3", 0)
+        place("h3", 0, 512, 128)
+        apply_gain(nc.vector, gains["h3"], "h3", 0, 128, 256)
+        apply_gain(nc.vector, gains["h3"], "h3", 0, 256, 512)
         tanh_pair("h3", 2, 0)
         tanh_pair("h3", 2, 1)
-        round_second("w5", w5_raw)
-        apply_gain("h3", 512, 256, 0)
-        quantize_h("h3", 256)
+        round_second(nc.scalar.copy, "w5", w5_raw)
+        quantize_second("w5")
+        quantize_h("h3", 0, 512)
+        gain_piece("h3", 512, 256, 128)
         tanh_pair("h1", 0, 0)
         tanh_pair("h1", 0, 1)
-        quantize_second("w5")
-        round_second("w4", w4_raw)
-        apply_gain("h1", 0, 256, 64)
-        quantize_h("h3", 512)
+        gain_piece("h1", 0, 256)
+        round_second(nc.vector.tensor_copy, "w4", w4_raw)
+        quantize_h("h3", 512, 256)
+        quantize_second("w4")
+        quantize_h("h1", 0, 256)
         tanh_pair("h1", 1, 0)
         tanh_pair("h1", 1, 1)
-        quantize_second("w4")
         park_y2(0, 256)
-        apply_gain("h1", 256, 256, 64)
-        quantize_h("h1", 0)
+        gain_piece("h1", 256, 256, 88)
+        multiply(0, 256)
+        quantize_h("h1", 256, 256)
         tanh_pair("h1", 2, 0)
         tanh_pair("h1", 2, 1)
         park_y2(256, 256)
-        apply_gain("h1", 512, 256, 96)
-        multiply(0, 256)
-        quantize_h("h1", 256)
+        gain_piece("h1", 512, 256, 128)
+        finish(0, 256)
+        multiply(256, 256)
+        quantize_h("h1", 512, 256)
         tanh_pair("h1", 3, 0)
         tanh_pair("h1", 3, 1)
         park_y2(512, 256)
-        finish(0, 256)
-        apply_gain("h1", 768, 256, 96)
-        multiply(256, 256)
-        quantize_h("h1", 512)
-        tanh_chunk("h3", 6)
-        tanh_chunk("h3", 7)
-        park_y2(768, 256)
+        gain_piece("h1", 768, 256, 128)
         finish(256, 256)
-        apply_gain("h3", 768, 128, 48)
         multiply(512, 256)
-        quantize_h("h1", 768)
-        finish(512, 256)
-        apply_gain("h3", 896, 128, 48)
-        quantize_h("h3", 768)
+        quantize_h("h1", 768, 256)
+        tanh_pair("h3", 3, 0)
+        tanh_pair("h3", 3, 1)
+        park_y2(768, 256)
+        gain_piece("h3", 768, 256, 88)
         multiply(768, 256)
-        quantize_h("h3", 896)
-        finish(768, 128)
-        finish(896, 128)
+        quantize_h("h3", 768, 256)
+        finish(512, 256)
+        finish(768, 256)

@@ -71,8 +71,9 @@ def tile_list_land_air_exchange_kernel(
             w2_raw[:].bitcast(I32).rearrange("p (a c) -> p a c", a=PASSES),
             w2_words.bitcast(I32).rearrange("a p c -> p a c"),
         )
-        nc.sync.dma_start(word_window[0][:].bitcast(I32), tab_words[0].rearrange("p t i -> p (t i)").bitcast(I32))
         for d in range(4):
+            if d == 3:
+                nc.sync.dma_start(word_window[0][:].bitcast(I32), tab_words[0].rearrange("p t i -> p (t i)").bitcast(I32))
             nc.sync.dma_start(
                 w2_scale_raw[32 * d : 32 * d + 4, :].bitcast(I32).rearrange("p (a c) -> p a c", a=PASSES),
                 w2_scales[:, 4 * d : 4 * d + 4, :].bitcast(I32).rearrange("a r c -> r a c"),
@@ -80,12 +81,12 @@ def tile_list_land_air_exchange_kernel(
         nc.sync.dma_start(
             gain2_rows[0:PACK, :].rearrange("t (b i) -> t b i", i=8), gain2.rearrange("(b t i) -> t b i", t=PACK, i=8)
         )
-        nc.sync.dma_start(word_window[1][:].bitcast(I32), tab_words[1].rearrange("p t i -> p (t i)").bitcast(I32))
         for d in range(4):
-            nc.gpsimd.dma_start(
+            nc.sync.dma_start(
                 w3_scale_raw[32 * d : 32 * d + 4 * PASSES, :].bitcast(I32),
                 w3_scales[:, 4 * d : 4 * d + 4, :].bitcast(I32),
             )
+        nc.sync.dma_start(word_window[1][:].bitcast(I32), tab_words[1].rearrange("p t i -> p (t i)").bitcast(I32))
 
         nc.gpsimd.memset(gain_rows[:], 0.0)
         nc.gpsimd.memset(w6_scale[:].bitcast(I32), 0)
@@ -194,12 +195,13 @@ def tile_list_land_air_exchange_kernel(
 
         second = {}
 
-        def round_second(copy, name, raw):
-            rounded = held([P, N, PACK], BF16, name + "_round")
+        def round_second(copy, name, raw, n0=0, n1=N):
+            if name not in second:
+                second[name] = held([P, N, PACK], BF16, name + "_round")
             copy(
-                rounded[:].rearrange("p (c i) t -> p c t i", i=4), raw[:].rearrange("p t (c i) -> p c t i", i=4)
+                second[name][:, n0:n1].rearrange("p (c i) t -> p c t i", i=4),
+                raw[:, :, n0:n1].rearrange("p t (c i) -> p c t i", i=4),
             )
-            second[name] = rounded
 
         def quantize_second(name):
             codes = held([P, N], U32, name + "_codes")
@@ -388,10 +390,10 @@ def tile_list_land_air_exchange_kernel(
         gain_piece("h3", 512, 256, 128)
         tanh_pair("h1", 0, 0)
         tanh_pair("h1", 0, 1)
+        round_second(nc.scalar.copy, "w4", w4_raw)
         gain_piece("h1", 0, 256)
-        round_second(nc.vector.tensor_copy, "w4", w4_raw)
-        quantize_h("h3", 512, 256)
         quantize_second("w4")
+        quantize_h("h3", 512, 256)
         quantize_h("h1", 0, 256)
         tanh_pair("h1", 1, 0)
         tanh_pair("h1", 1, 1)

@@ -98,7 +98,7 @@ def tile_list_land_air_exchange_kernel(
         gains["h2"] = gain2_bank[:, 0:PACK]
         gain_copy = held([P, 12], F32, "gain_copy", 16384)
         gain_columns = {name: gain_copy[:, at : at + PACK] for name, at in gain_at.items()}
-        gain2_copy = held([P, PACK], F32, "gain2_copy")
+        gain2_copy = held([P, PACK], F32, "gain2_copy", 8192)
         nc.vector.tensor_copy(gain2_copy[:], gains["h2"])
         gain_columns["h2"] = gain2_copy[:]
 
@@ -357,8 +357,8 @@ def tile_list_land_air_exchange_kernel(
         quantize_h("h2", 0, 256)
         tanh_chunk("h2", 2)
         tanh_chunk("h2", 3)
-        place("h2", 256, 512, 128)
-        apply_gain(nc.vector, gains["h2"], "h2", 256, 128, 256)
+        place("h2", 256, 512, 120)
+        apply_gain(nc.vector, gains["h2"], "h2", 256, 120, 256)
         tanh_chunk("h2", 4)
         tanh_chunk("h2", 5)
         apply_gain(nc.vector, gains["h2"], "h2", 256, 256, 512)
@@ -366,11 +366,10 @@ def tile_list_land_air_exchange_kernel(
         tanh_chunk("h2", 6)
         round_w1(nc.scalar.copy, 0, 1, 2)
         tanh_chunk("h2", 7)
-        round_w1(nc.scalar.copy, 0, 2, 3)
+        round_w1(nc.vector.tensor_copy, 0, 2, 4)
         round_w1(nc.vector.tensor_copy, 1, 0, 4)
         quantize_h("h2", 256, 512)
         gain_piece("h2", 768, 256, 40)
-        round_w1(nc.scalar.copy, 0, 3, 4)
         quantize_w1(1)
         quantize_w1(0)
         quantize_h("h2", 768, 256)
@@ -379,15 +378,15 @@ def tile_list_land_air_exchange_kernel(
         copy_gains()
         tanh_pair("h3", 1, 0)
         tanh_pair("h3", 1, 1)
-        place("h3", 0, 512, 128)
-        apply_gain(nc.vector, gains["h3"], "h3", 0, 128, 256)
+        place("h3", 0, 512, 120)
+        apply_gain(nc.vector, gains["h3"], "h3", 0, 120, 256)
         apply_gain(nc.vector, gains["h3"], "h3", 0, 256, 512)
         tanh_pair("h3", 2, 0)
         tanh_pair("h3", 2, 1)
         round_second(nc.scalar.copy, "w5", w5_raw)
         quantize_second("w5")
         quantize_h("h3", 0, 512)
-        gain_piece("h3", 512, 256, 128)
+        gain_piece("h3", 512, 256, 120)
         tanh_pair("h1", 0, 0)
         tanh_pair("h1", 0, 1)
         round_second(nc.scalar.copy, "w4", w4_raw)
@@ -398,27 +397,27 @@ def tile_list_land_air_exchange_kernel(
         tanh_pair("h1", 1, 0)
         tanh_pair("h1", 1, 1)
         park_y2(0, 256)
-        gain_piece("h1", 256, 256, 88)
+        gain_piece("h1", 256, 256, 80)
         multiply(0, 256)
         quantize_h("h1", 256, 256)
         tanh_pair("h1", 2, 0)
         tanh_pair("h1", 2, 1)
         park_y2(256, 256)
-        gain_piece("h1", 512, 256, 128)
+        gain_piece("h1", 512, 256, 120)
         finish(0, 256)
         multiply(256, 256)
         quantize_h("h1", 512, 256)
         tanh_pair("h1", 3, 0)
         tanh_pair("h1", 3, 1)
         park_y2(512, 256)
-        gain_piece("h1", 768, 256, 128)
+        gain_piece("h1", 768, 256, 120)
         finish(256, 256)
         multiply(512, 256)
         quantize_h("h1", 768, 256)
         tanh_pair("h3", 3, 0)
         tanh_pair("h3", 3, 1)
         park_y2(768, 256)
-        gain_piece("h3", 768, 256, 88)
+        gain_piece("h3", 768, 256, 80)
         multiply(768, 256)
         quantize_h("h3", 768, 256)
         finish(512, 256)

@@ -167,8 +167,8 @@ def tile_list_land_air_exchange_kernel(
 
         def order_w3():
             nc.vector.tensor_copy(
-                w3_codes[:].rearrange("p (a t m) -> p a m t", a=PASSES, t=PACK),
-                w3_raw[:].rearrange("p (a m t) -> p a m t", a=PASSES, t=PACK),
+                w3_codes[:].rearrange("p (a t b i) -> p a b t i", a=PASSES, t=PACK, i=4),
+                w3_raw[:].rearrange("p (a b i t) -> p a b t i", a=PASSES, t=PACK, i=4),
             )
 
         def order_w3_scale():
@@ -366,10 +366,11 @@ def tile_list_land_air_exchange_kernel(
         tanh_chunk("h2", 6)
         round_w1(nc.scalar.copy, 0, 1, 2)
         tanh_chunk("h2", 7)
-        round_w1(nc.vector.tensor_copy, 0, 2, 4)
+        round_w1(nc.scalar.copy, 0, 2, 3)
         round_w1(nc.vector.tensor_copy, 1, 0, 4)
         quantize_h("h2", 256, 512)
         gain_piece("h2", 768, 256, 40)
+        round_w1(nc.scalar.copy, 0, 3, 4)
         quantize_w1(1)
         quantize_w1(0)
         quantize_h("h2", 768, 256)

@@ -127,7 +127,19 @@ def tile_list_land_air_exchange_kernel(
             w2_codes[:].bitcast(I32).rearrange("p (a t b w) -> p a t b w", a=PASSES, t=PACK, w=4),
             w2_raw[:].bitcast(I32).rearrange("p (a b t w) -> p a t b w", a=PASSES, t=PACK, w=4),
         )
-        gather_words(0, 0, S)
+        gather_words(0, 0, QUARTER)
+        warm_bank = first_banks.tile([P, 2, QUARTER], F32, name="first_bank")
+        for n in range(6):
+            nc.tensor.matmul_mx(
+                warm_bank[:, n % 2, :],
+                lhsT=v_codes[0][:, 0:P].bitcast(E4M3),
+                lhsT_scale=picked_scale[:, 0:P],
+                rhs=v_codes[0][:, 0:QUARTER].bitcast(E4M3),
+                rhs_scale=picked_scale[:, 0:QUARTER],
+                start=(n == 0),
+                stop=(n == 5),
+            )
+        gather_words(0, QUARTER, S)
         nc.vector.tensor_copy(
             w2_scale[:].bitcast(I32).rearrange("p (a t b w) -> p a t b w", a=PASSES, t=PACK, w=2),
             w2_scale_raw[:].bitcast(I32).rearrange("p (a b t w) -> p a t b w", a=PASSES, t=PACK, w=2),
@@ -142,7 +154,7 @@ def tile_list_land_air_exchange_kernel(
         w5_raw = held([P, PACK, N], F32, "w5_raw", 30592)
         w4_raw = held([P, PACK, N], F32, "w4_raw", 35584)
         w1_rows = w1.rearrange("(a p j) r -> a p j r", a=PASSES, j=PACK)
-        nc.sync.dma_start(
+        nc.gpsimd.dma_start(
             w3_raw[:].rearrange("p (a c) -> p a c", a=PASSES),
             w3_words.rearrange("a p c i -> p a (c i)").bitcast(I32),
         )
@@ -162,7 +174,8 @@ def tile_list_land_air_exchange_kernel(
                 w6_scale[32 * d : 32 * d + 4, :].bitcast(I32), w6_scales[0, 4 * d : 4 * d + 4, :].bitcast(I32)
             )
 
-        w3_codes = held([P, PASSES * H], I32, "w3_codes")
+        first_tanh = held([P, QUARTER * PACK], F32, "first_tanh", 39680)
+        w3_codes = held([P, PASSES * H], I32, "w3_codes", 39680)
         w3_scale = held([P, H], U8, "w3_scale", 16448)
 
         def order_w3():
@@ -233,6 +246,10 @@ def tile_list_land_air_exchange_kernel(
         stage_end = [0]
         placed = {}
 
+        def tanh_words(name, j0, j1):
+            tile = first_tanh if name == "h2" and j1 <= QUARTER else tanhs[name]
+            return tile[:, PACK * j0 : PACK * j1]
+
         def by_slot(run):
             return run.rearrange("p (j t) -> p j t", t=PACK)
 
@@ -252,7 +269,7 @@ def tile_list_land_air_exchange_kernel(
                         stop=(a == PASSES - 1 and t == PACK - 1),
                     )
             nc.scalar.activation(
-                by_slot(tanhs[name][:, PACK * j0 : PACK * (j0 + CHUNK)]), bank[:].rearrange("p t j -> p j t"), TANH
+                by_slot(tanh_words(name, j0, j0 + CHUNK)), bank[:].rearrange("p t j -> p j t"), TANH
             )
 
         def tanh_pair(name, quarter, u):
@@ -281,7 +298,7 @@ def tile_list_land_air_exchange_kernel(
         def tanh_columns(name, start, c0, c1):
             if (name, start) in paired:
                 return pairs[name][:].rearrange("p (u j e) -> p j u e", u=2, e=2)[:, start + c0 : start + c1]
-            return tanhs[name][:, PACK * (start + c0) : PACK * (start + c1)].rearrange("p (j u e) -> p j u e", u=2, e=2)
+            return tanh_words(name, start + c0, start + c1).rearrange("p (j u e) -> p j u e", u=2, e=2)
 
         def place(name, start, width, share=0):
             at = stage_end[0] - PACK * share

@@ -21,7 +21,6 @@ ADD = mybir.AluOpType.add
 P = 128
 PACK = 4
 PASSES = K // (P * PACK)
-CHUNK = 128
 QUARTER = 256
 HALVES = N // P
 
@@ -48,36 +47,42 @@ def tile_list_land_air_exchange_kernel(
         nc.sync.dma_start(offsets[:], offs)
 
         scale_window = held([P, T], U8, "scale_window")
-        for a in range(PASSES):
-            nc.sync.dma_start(
-                scale_window[a:P:PASSES, :].bitcast(I32),
-                tab_scales[a].bitcast(I32).unsqueeze(1).to_broadcast([16, 4, T // 4]),
-            )
-        word_window = [held([P, T], U32, "word_window%d" % a, 8192 * a) for a in range(PASSES)]
-        w2_raw = held([P, PASSES * H * 2], U8, "w2_raw", 20416)
+        word_window = [held([P, T], U32, "word_window%d" % a, (45696, 18304)[a]) for a in range(PASSES)]
+        w2_raw = held([P, PASSES * H * 2], U8, "w2_raw", 8128)
         w2_scale_raw = held([P, PASSES * H], U8, "w2_scale_raw")
         w3_scale_raw = held([P, H], U8, "w3_scale_raw")
         w6_scale = held([P, N], U8, "w6_scale")
-        gain2_rows = held([P, P], F32, "gain2_rows")
         gain_rows = held([P, H], F32, "gain_rows")
+        gain2_rows = held([P, P], F32, "gain2_rows")
         identity = held([P, P], F32, "identity")
         v_scale = held([P, PASSES * S], U8, "v_scale")
         nc.gpsimd.memset(w2_scale_raw[:].bitcast(I32), 0)
         nc.gpsimd.memset(gain2_rows[:], 0.0)
         nc.gpsimd.memset(w3_scale_raw[:].bitcast(I32), 0)
-        make_identity(nc, identity[:])
         nc.vector.memset(v_scale[:, S:].bitcast(I32), 0)
-        nc.sync.dma_start(
-            w2_raw[:].bitcast(I32).rearrange("p (a c) -> p a c", a=PASSES),
-            w2_words.bitcast(I32).rearrange("a p c -> p a c"),
-        )
-        for d in range(4):
-            if d == 3:
-                nc.sync.dma_start(word_window[0][:].bitcast(I32), tab_words[0].rearrange("p t i -> p (t i)").bitcast(I32))
+
+        def load_w2_scale(d):
             nc.sync.dma_start(
                 w2_scale_raw[32 * d : 32 * d + 4, :].bitcast(I32).rearrange("p (a c) -> p a c", a=PASSES),
                 w2_scales[:, 4 * d : 4 * d + 4, :].bitcast(I32).rearrange("a r c -> r a c"),
             )
+
+        def load_words(a):
+            nc.sync.dma_start(word_window[a][:].bitcast(I32), tab_words[a].rearrange("p t i -> p (t i)").bitcast(I32))
+
+        for a in range(PASSES):
+            nc.sync.dma_start(
+                scale_window[a:P:PASSES, :].bitcast(I32),
+                tab_scales[a].bitcast(I32).unsqueeze(1).to_broadcast([16, 4, T // 4]),
+            )
+        nc.sync.dma_start(
+            w2_raw[:].bitcast(I32).rearrange("p (a c) -> p a c", a=PASSES),
+            w2_words.bitcast(I32).rearrange("a p c -> p a c"),
+        )
+        for d in range(3):
+            load_w2_scale(d)
+        load_words(0)
+        load_w2_scale(3)
         nc.sync.dma_start(
             gain2_rows[0:PACK, :].rearrange("t (b i) -> t b i", i=8), gain2.rearrange("(b t i) -> t b i", t=PACK, i=8)
         )
@@ -86,23 +91,23 @@ def tile_list_land_air_exchange_kernel(
                 w3_scale_raw[32 * d : 32 * d + 4 * PASSES, :].bitcast(I32),
                 w3_scales[:, 4 * d : 4 * d + 4, :].bitcast(I32),
             )
-        nc.sync.dma_start(word_window[1][:].bitcast(I32), tab_words[1].rearrange("p t i -> p (t i)").bitcast(I32))
-
+        load_words(1)
+        make_identity(nc, identity[:])
         nc.gpsimd.memset(gain_rows[:], 0.0)
         nc.gpsimd.memset(w6_scale[:].bitcast(I32), 0)
+
         gain2_bank = second_banks.tile([P, P], F32, name="second_bank")
         nc.tensor.transpose(gain2_bank[:], gain2_rows[:], identity[:])
         gain_bank = gain_banks.tile([P, PACK + P], F32, name="gain_bank")
         gain_at = {"h3": 0, "h1": 8}
         gains = {name: gain_bank[:, at : at + PACK] for name, at in gain_at.items()}
         gains["h2"] = gain2_bank[:, 0:PACK]
-        gain_copy = held([P, 12], F32, "gain_copy", 16384)
+        gain_copy = held([P, 12], F32, "gain_copy")
+        gain2_copy = held([P, PACK], F32, "gain2_copy", 18304)
         gain_columns = {name: gain_copy[:, at : at + PACK] for name, at in gain_at.items()}
-        gain2_copy = held([P, PACK], F32, "gain2_copy", 8192)
-        nc.vector.tensor_copy(gain2_copy[:], gains["h2"])
         gain_columns["h2"] = gain2_copy[:]
 
-        def copy_gains():
+        def turn_gains():
             for t in range(PACK):
                 nc.tensor.transpose(gain_bank[:, t : t + P], gain_rows[:, t:H:PACK], identity[:])
             nc.tensor.transpose(gain_bank[:, PACK : PACK + P], gain_rows[:, 0:P], identity[:])
@@ -147,12 +152,13 @@ def tile_list_land_air_exchange_kernel(
         gather_words(1, 0, QUARTER)
         gather_words(1, QUARTER, 2 * QUARTER)
         gather_words(1, 2 * QUARTER, S)
+        nc.vector.tensor_copy(gain2_copy[:], gains["h2"])
 
-        w1_raw = [held([P, PACK, H], F32, "w1_raw%d" % a, (22400, 0)[a]) for a in range(PASSES)]
-        w3_raw = held([P, PASSES * H], I32, "w3_raw", 16384)
+        w1_raw = [held([P, PACK, H], F32, "w1_raw%d" % a, (10112, 45696)[a]) for a in range(PASSES)]
+        w3_raw = held([P, PASSES * H], I32, "w3_raw", 4096)
         w6_codes = held([P, 2 * N], U8, "w6_codes", 34944)
-        w5_raw = held([P, PACK, N], F32, "w5_raw", 30592)
-        w4_raw = held([P, PACK, N], F32, "w4_raw", 35584)
+        w5_raw = held([P, PACK, N], F32, "w5_raw", 35584)
+        w4_raw = held([P, PACK, N], F32, "w4_raw", 30592)
         w1_rows = w1.rearrange("(a p j) r -> a p j r", a=PASSES, j=PACK)
         nc.gpsimd.dma_start(
             w3_raw[:].rearrange("p (a c) -> p a c", a=PASSES),
@@ -162,34 +168,31 @@ def tile_list_land_air_exchange_kernel(
             nc.sync.dma_start(w1_raw[a][:], w1_rows[a])
         nc.sync.dma_start(gain_rows[0:1, :], gain3.unsqueeze(0))
         nc.sync.dma_start(
-            gain_rows[4:8, 0:P].rearrange("t (e i) -> t e i", i=4), gain1.rearrange("(e t i) -> t e i", t=PACK, i=4)
+            gain_rows[4:8, 0:P].rearrange("t (b i) -> t b i", i=4), gain1.rearrange("(b t i) -> t b i", t=PACK, i=4)
         )
-        for t in range(PACK):
-            nc.sync.dma_start(w5_raw[:, t, :], w5.rearrange("(b t i) n -> t b i n", t=PACK, i=8)[t])
-        for t in range(PACK):
-            nc.sync.dma_start(w4_raw[:, t, :], w4.rearrange("(e t i) n -> t e i n", t=PACK, i=4)[t])
+        for raw, w, run in ((w5_raw, w5, 8), (w4_raw, w4, 4)):
+            for t in range(PACK):
+                nc.sync.dma_start(raw[:, t, :], w.rearrange("(b t i) n -> t b i n", t=PACK, i=run)[t])
         nc.sync.dma_start(w6_codes[:].bitcast(I32), w6_words[0].bitcast(I32))
         for d in range(4):
             nc.sync.dma_start(
                 w6_scale[32 * d : 32 * d + 4, :].bitcast(I32), w6_scales[0, 4 * d : 4 * d + 4, :].bitcast(I32)
             )
 
-        first_tanh = held([P, QUARTER * PACK], F32, "first_tanh", 39680)
-        w3_codes = held([P, PASSES * H], I32, "w3_codes", 39680)
-        w3_scale = held([P, H], U8, "w3_scale", 16448)
+        first_pairs = held([P, 2 * QUARTER * 2], F32, "first_pairs", 0)
+        w3_codes = held([P, PASSES * H], I32, "w3_codes", 0)
+        w3_scale = held([P, H], U8, "w3_scale", 4096)
 
         def order_w3():
             nc.vector.tensor_copy(
                 w3_codes[:].rearrange("p (a t b i) -> p a b t i", a=PASSES, t=PACK, i=4),
                 w3_raw[:].rearrange("p (a b i t) -> p a b t i", a=PASSES, t=PACK, i=4),
             )
-
-        def order_w3_scale():
             nc.vector.tensor_copy(
                 w3_scale[:].rearrange("p (t m) -> p t m", t=PACK), w3_scale_raw[:].rearrange("p (m t) -> p t m", t=PACK)
             )
 
-        w1_round = [held([P, PACK, P, PACK], BF16, "w1_round%d" % a) for a in range(PASSES)]
+        w1_round = [held([P, PACK, P, PACK], BF16, "w1_round%d" % a, 61440 + 4096 * a) for a in range(PASSES)]
         w1_codes = held([P, PASSES * H], U32, "w1_codes")
         w1_scale = held([P, PASSES * H], U8, "w1_scale")
 
@@ -206,21 +209,21 @@ def tile_list_land_air_exchange_kernel(
                 w1_round[a][:].rearrange("p t m j -> p (t m j)"),
             )
 
-        second = {}
+        raws = {"w4": w4_raw, "w5": w5_raw}
+        rounded = {name: held([P, N, PACK], BF16, name + "_round") for name in raws}
+        second_codes = {name: held([P, N], U32, name + "_codes") for name in raws}
+        second_scale = {name: held([P, N], U8, name + "_scale") for name in raws}
 
-        def round_second(copy, name, raw, n0=0, n1=N):
-            if name not in second:
-                second[name] = held([P, N, PACK], BF16, name + "_round")
+        def round_second(copy, name):
             copy(
-                second[name][:, n0:n1].rearrange("p (c i) t -> p c t i", i=4),
-                raw[:, :, n0:n1].rearrange("p t (c i) -> p c t i", i=4),
+                rounded[name][:].rearrange("p (c i) t -> p c t i", i=4),
+                raws[name][:].rearrange("p t (c i) -> p c t i", i=4),
             )
 
         def quantize_second(name):
-            codes = held([P, N], U32, name + "_codes")
-            scale = held([P, N], U8, name + "_scale")
-            nc.vector.quantize_mx(codes[:].bitcast(E4M3), scale[:], second[name][:].rearrange("p n t -> p (n t)"))
-            second[name] = (codes, scale)
+            nc.vector.quantize_mx(
+                second_codes[name][:].bitcast(E4M3), second_scale[name][:], rounded[name][:].rearrange("p n t -> p (n t)")
+            )
 
         def first_weight(name, a, t):
             c0 = a * H + t * P
@@ -233,29 +236,30 @@ def tile_list_land_air_exchange_kernel(
         def second_weight(name, u):
             if name == "h3":
                 return w6_codes[:, 2 * u * P : 2 * (u + 1) * P].bitcast(E2M1), w6_scale[:, u * P : (u + 1) * P]
-            codes, scale = second["w4" if name == "h1" else "w5"]
-            return codes[:, u * P : (u + 1) * P].bitcast(E4M3), scale[:, u * P : (u + 1) * P]
+            w = "w4" if name == "h1" else "w5"
+            return second_codes[w][:, u * P : (u + 1) * P].bitcast(E4M3), second_scale[w][:, u * P : (u + 1) * P]
 
         names = ("h1", "h2", "h3")
-        h_codes = {name: held([P, S], U32, name + "_codes") for name in names}
-        h_scale = {name: held([P, S], U8, name + "_scale") for name in names}
-        tanhs = {name: held([P, S * PACK], F32, name + "_tanh") for name in ("h2", "h3")}
-        pairs = {name: held([P, S * PACK], F32, name + "_pairs") for name in ("h1", "h3")}
-        paired = set()
+        quantized = {}
+        pairs = {}
         stage = held([P, 3 * S * PACK], BF16, "stage")
         stage_end = [0]
         placed = {}
+        chunked = set()
+        words = {}
 
-        def tanh_words(name, j0, j1):
-            tile = first_tanh if name == "h2" and j1 <= QUARTER else tanhs[name]
-            return tile[:, PACK * j0 : PACK * j1]
+        def tanh_view(name, j0, j1):
+            if name == "h2" and j1 <= QUARTER:
+                return first_pairs[:].rearrange("p (j u e) -> p u j e", u=2, e=2)[:, :, j0:j1]
+            if (name, j0 // QUARTER) in chunked:
+                return words[name][:].rearrange("p (j u e) -> p u j e", u=2, e=2)[:, :, j0:j1]
+            q = j0 // QUARTER
+            return pairs[name, q][:, :, j0 - q * QUARTER : j1 - q * QUARTER]
 
-        def by_slot(run):
-            return run.rearrange("p (j t) -> p j t", t=PACK)
-
-        def tanh_chunk(name, chunk):
-            bank = first_banks.tile([P, PACK, CHUNK], F32, name="first_bank")
-            j0 = chunk * CHUNK
+        def tanh_chunk(name, j0):
+            bank = first_banks.tile([P, PACK, P], F32, name="first_bank")
+            chunked.add((name, j0 // QUARTER))
+            tile = first_pairs
             for a in range(PASSES):
                 for t in range(PACK):
                     codes, scale = first_weight(name, a, t)
@@ -263,179 +267,179 @@ def tile_list_land_air_exchange_kernel(
                         bank[:, t, :],
                         lhsT=codes,
                         lhsT_scale=scale,
-                        rhs=v_codes[a][:, j0 : j0 + CHUNK].bitcast(E4M3),
-                        rhs_scale=v_scale[:, a * S + j0 : a * S + j0 + CHUNK],
+                        rhs=v_codes[a][:, j0 : j0 + P].bitcast(E4M3),
+                        rhs_scale=v_scale[:, a * S + j0 : a * S + j0 + P],
                         start=(a == 0 and t == 0),
                         stop=(a == PASSES - 1 and t == PACK - 1),
                     )
             nc.scalar.activation(
-                by_slot(tanh_words(name, j0, j0 + CHUNK)), bank[:].rearrange("p t j -> p j t"), TANH
-            )
-
-        def tanh_pair(name, quarter, u):
-            bank = first_banks.tile([P, 2, QUARTER], F32, name="first_bank")
-            j0 = quarter * QUARTER
-            paired.add((name, j0))
-            for a in range(PASSES):
-                for e in range(2):
-                    codes, scale = first_weight(name, a, 2 * u + e)
-                    nc.tensor.matmul_mx(
-                        bank[:, e, :],
-                        lhsT=codes,
-                        lhsT_scale=scale,
-                        rhs=v_codes[a][:, j0 : j0 + QUARTER].bitcast(E4M3),
-                        rhs_scale=v_scale[:, a * S + j0 : a * S + j0 + QUARTER],
-                        start=(a == 0 and e == 0),
-                        stop=(a == PASSES - 1 and e == 1),
-                    )
-            c0 = 2 * (u * S + j0)
-            nc.scalar.activation(
-                pairs[name][:, c0 : c0 + 2 * QUARTER].rearrange("p (j e) -> p j e", e=2),
-                bank[:].rearrange("p e j -> p j e"),
+                tile[:, PACK * j0 : PACK * (j0 + P)].rearrange("p (j t) -> p j t", t=PACK),
+                bank[:].rearrange("p t j -> p j t"),
                 TANH,
             )
 
-        def tanh_columns(name, start, c0, c1):
-            if (name, start) in paired:
-                return pairs[name][:].rearrange("p (u j e) -> p j u e", u=2, e=2)[:, start + c0 : start + c1]
-            return tanh_words(name, start + c0, start + c1).rearrange("p (j u e) -> p j u e", u=2, e=2)
-
-        def place(name, start, width, share=0):
-            at = stage_end[0] - PACK * share
-            stage_end[0] = at + PACK * width
-            placed[name, start] = at
-            if share:
-                apply_gain(nc.gpsimd, gain_columns[name], name, start, 0, share)
+        def tanh_quarter(name, quarter, halves=(0, 1), on=None):
+            j0 = quarter * QUARTER
+            if (name, quarter) not in pairs:
+                pairs[name, quarter] = held([P, 2, QUARTER, 2], F32, "%s_pairs%d" % (name, quarter), on)
+            for u in halves:
+                bank = first_banks.tile([P, 2, QUARTER], F32, name="first_bank")
+                for a in range(PASSES):
+                    for e in range(2):
+                        codes, scale = first_weight(name, a, 2 * u + e)
+                        nc.tensor.matmul_mx(
+                            bank[:, e, :],
+                            lhsT=codes,
+                            lhsT_scale=scale,
+                            rhs=v_codes[a][:, j0 : j0 + QUARTER].bitcast(E4M3),
+                            rhs_scale=v_scale[:, a * S + j0 : a * S + j0 + QUARTER],
+                            start=(a == 0 and e == 0),
+                            stop=(a == PASSES - 1 and e == 1),
+                        )
+                nc.scalar.activation(
+                    tanh_view(name, j0, j0 + QUARTER)[:, u], bank[:].rearrange("p e j -> p j e"), TANH
+                )
 
         def apply_gain(engine, gain, name, start, c0, c1):
-            at = placed[name, start]
             engine.tensor_tensor(
-                stage[:, at + PACK * c0 : at + PACK * c1].rearrange("p (j u e) -> p j u e", u=2, e=2),
-                tanh_columns(name, start, c0, c1),
+                placed[name, start][:, PACK * c0 : PACK * c1].rearrange("p (j u e) -> p j u e", u=2, e=2),
+                tanh_view(name, start + c0, start + c1).rearrange("p u j e -> p j u e"),
                 gain.rearrange("p (u e) -> p u e", e=2).unsqueeze(1).to_broadcast([P, c1 - c0, 2, 2]),
                 MULT,
             )
 
-        def gain_piece(name, start, width, share=0):
-            place(name, start, width, share)
-            apply_gain(nc.vector, gains[name], name, start, share, width)
+        def place(name, start, width, share, on=None):
+            if on is None:
+                at = stage_end[0] - PACK * share
+                stage_end[0] = at + PACK * width
+                placed[name, start] = stage[:, at : at + PACK * width]
+            else:
+                placed[name, start] = held([P, PACK * width], BF16, "%s_stage%d" % (name, start), on)[:]
+            if share:
+                apply_gain(nc.gpsimd, gain_columns[name], name, start, 0, share)
 
-        def quantize_h(name, start, width):
-            at = placed[name, start]
-            nc.vector.quantize_mx(
-                h_codes[name][:, start : start + width].bitcast(E4M3),
-                h_scale[name][:, start : start + width],
-                stage[:, at : at + PACK * width],
-            )
+        def own_gain(name, start, c0, c1):
+            apply_gain(nc.vector, gains[name], name, start, c0, c1)
+
+        def gain_piece(name, start, width, share, on=None):
+            place(name, start, width, share, on)
+            own_gain(name, start, share, width)
+
+        def quantize_h(name, start, width, on=None):
+            codes = held([P, width], U32, "%s_codes%d" % (name, start), on)
+            scale = held([P, width], U8, "%s_scale%d" % (name, start))
+            nc.vector.quantize_mx(codes[:].bitcast(E4M3), scale[:], placed[name, start])
+            for c0 in range(0, width, P):
+                quantized[name, start + c0] = (codes, scale, c0)
 
         def second_stage(name, start, width):
             bank = second_banks.tile([P, HALVES, width], F32, name="second_bank")
+            h_codes, h_scale, c0 = quantized[name, start]
             for u in range(HALVES):
                 codes, scale = second_weight(name, u)
                 nc.tensor.matmul_mx(
                     bank[:, u, :],
                     lhsT=codes,
                     lhsT_scale=scale,
-                    rhs=h_codes[name][:, start : start + width].bitcast(E4M3),
-                    rhs_scale=h_scale[name][:, start : start + width],
+                    rhs=h_codes[:, c0 : c0 + width].bitcast(E4M3),
+                    rhs_scale=h_scale[:, c0 : c0 + width],
                     start=True,
                     stop=True,
                 )
             return bank
 
-        y2 = held([P, HALVES, S], F32, "y2")
-        product = held([P, HALVES, S], F32, "product")
+        y2 = {q * QUARTER: held([P, HALVES, QUARTER], F32, "y2_%d" % q, 79872 + 2048 * q) for q in range(4)}
+        product = {q * QUARTER: held([P, HALVES, QUARTER], F32, "product%d" % q, 69632 + 2048 * q) for q in range(4)}
 
         def park_y2(start, width):
-            nc.scalar.copy(y2[:, :, start : start + width], second_stage("h2", start, width)[:])
+            nc.scalar.copy(y2[start][:], second_stage("h2", start, width)[:])
 
         def multiply(start, width):
             nc.vector.tensor_tensor(
-                product[:, :, start : start + width],
+                product[start][:],
                 second_stage("h1", start, width)[:],
-                y2[:, :, start : start + width],
+                y2[start][:],
                 MULT,
             )
 
         def finish(start, width):
             result = ring.tile([P, HALVES, width], F32, name="result")
             nc.vector.tensor_tensor(
-                result[:], second_stage("h3", start, width)[:], product[:, :, start : start + width], ADD
+                result[:], second_stage("h3", start, width)[:], product[start][:], ADD
             )
             nc.sync.dma_start(out.rearrange("(u p) j -> p u j", p=P)[:, :, start : start + width], result[:])
 
         tanh_chunk("h2", 0)
-        place("h2", 0, 256)
-        apply_gain(nc.vector, gains["h2"], "h2", 0, 0, 128)
-        tanh_chunk("h2", 1)
-        apply_gain(nc.vector, gains["h2"], "h2", 0, 128, 256)
+        place("h2", 0, 256, 0, None)
+        own_gain("h2", 0, 0, 128)
+        tanh_chunk("h2", 128)
+        own_gain("h2", 0, 128, 256)
         order_w3()
-        order_w3_scale()
         quantize_h("h2", 0, 256)
-        tanh_chunk("h2", 2)
-        tanh_chunk("h2", 3)
-        place("h2", 256, 512, 120)
-        apply_gain(nc.vector, gains["h2"], "h2", 256, 120, 256)
-        tanh_chunk("h2", 4)
-        tanh_chunk("h2", 5)
-        apply_gain(nc.vector, gains["h2"], "h2", 256, 256, 512)
+        tanh_quarter("h2", 1, (0,))
+        tanh_quarter("h2", 1, (1,))
+        place("h2", 256, 512, 120, None)
+        own_gain("h2", 256, 120, 256)
+        tanh_quarter("h2", 2, (0,))
+        tanh_quarter("h2", 2, (1,))
+        own_gain("h2", 256, 256, 512)
         round_w1(nc.scalar.copy, 0, 0, 1)
-        tanh_chunk("h2", 6)
+        tanh_quarter("h2", 3, (0,))
         round_w1(nc.scalar.copy, 0, 1, 2)
-        tanh_chunk("h2", 7)
+        tanh_quarter("h2", 3, (1,))
         round_w1(nc.scalar.copy, 0, 2, 3)
         round_w1(nc.vector.tensor_copy, 1, 0, 4)
         quantize_h("h2", 256, 512)
-        gain_piece("h2", 768, 256, 40)
+        gain_piece("h2", 768, 256, 40, None)
         round_w1(nc.scalar.copy, 0, 3, 4)
         quantize_w1(1)
         quantize_w1(0)
         quantize_h("h2", 768, 256)
-        tanh_pair("h3", 0, 0)
-        tanh_pair("h3", 0, 1)
-        copy_gains()
-        tanh_pair("h3", 1, 0)
-        tanh_pair("h3", 1, 1)
-        place("h3", 0, 512, 120)
-        apply_gain(nc.vector, gains["h3"], "h3", 0, 120, 256)
-        apply_gain(nc.vector, gains["h3"], "h3", 0, 256, 512)
-        tanh_pair("h3", 2, 0)
-        tanh_pair("h3", 2, 1)
-        round_second(nc.scalar.copy, "w5", w5_raw)
+        tanh_quarter("h3", 0, (0,))
+        tanh_quarter("h3", 0, (1,))
+        turn_gains()
+        tanh_quarter("h3", 1, (0,))
+        tanh_quarter("h3", 1, (1,))
+        place("h3", 0, 512, 120, None)
+        own_gain("h3", 0, 120, 256)
+        own_gain("h3", 0, 256, 512)
+        tanh_quarter("h3", 2, (0,))
+        tanh_quarter("h3", 2, (1,))
+        round_second(nc.scalar.copy, "w5")
         quantize_second("w5")
         quantize_h("h3", 0, 512)
-        gain_piece("h3", 512, 256, 120)
-        tanh_pair("h1", 0, 0)
-        tanh_pair("h1", 0, 1)
-        round_second(nc.scalar.copy, "w4", w4_raw)
-        gain_piece("h1", 0, 256)
+        gain_piece("h3", 512, 256, 120, None)
+        tanh_quarter("h1", 0, (0,))
+        tanh_quarter("h1", 0, (1,))
+        round_second(nc.scalar.copy, "w4")
+        gain_piece("h1", 0, 256, 0, None)
         quantize_second("w4")
         quantize_h("h3", 512, 256)
         quantize_h("h1", 0, 256)
-        tanh_pair("h1", 1, 0)
-        tanh_pair("h1", 1, 1)
+        tanh_quarter("h1", 1, (0,))
+        tanh_quarter("h1", 1, (1,))
         park_y2(0, 256)
-        gain_piece("h1", 256, 256, 80)
+        gain_piece("h1", 256, 256, 80, None)
         multiply(0, 256)
         quantize_h("h1", 256, 256)
-        tanh_pair("h1", 2, 0)
-        tanh_pair("h1", 2, 1)
+        tanh_quarter("h1", 2, (0,))
+        tanh_quarter("h1", 2, (1,))
         park_y2(256, 256)
-        gain_piece("h1", 512, 256, 120)
+        gain_piece("h1", 512, 256, 152, 79872)
         finish(0, 256)
         multiply(256, 256)
         quantize_h("h1", 512, 256)
-        tanh_pair("h1", 3, 0)
-        tanh_pair("h1", 3, 1)
+        tanh_quarter("h1", 3, (0,))
+        tanh_quarter("h1", 3, (1,))
         park_y2(512, 256)
-        gain_piece("h1", 768, 256, 120)
+        gain_piece("h1", 768, 256, 152, 81920)
         finish(256, 256)
         multiply(512, 256)
         quantize_h("h1", 768, 256)
-        tanh_pair("h3", 3, 0)
-        tanh_pair("h3", 3, 1)
+        tanh_quarter("h3", 3, (0,))
+        tanh_quarter("h3", 3, (1,))
         park_y2(768, 256)
-        gain_piece("h3", 768, 256, 80)
+        gain_piece("h3", 768, 256, 104, 83968)
         multiply(768, 256)
         quantize_h("h3", 768, 256)
         finish(512, 256)

@@ -192,7 +192,21 @@ def tile_list_land_air_exchange_kernel(
                 w3_scale[:].rearrange("p (t m) -> p t m", t=PACK), w3_scale_raw[:].rearrange("p (m t) -> p t m", t=PACK)
             )
 
-        w1_round = [held([P, PACK, P, PACK], BF16, "w1_round%d" % a, 61440 + 4096 * a) for a in range(PASSES)]
+        arena = held([P, 37 * S], BF16, "arena")
+        arena_end = [0]
+        ends = {}
+
+        def take(key, count, back=0, behind=None):
+            at = (arena_end[0] if behind is None else ends[behind]) - back
+            ends[key] = at + count
+            if behind is None:
+                arena_end[0] = at + count + 2 * PACK * QUARTER
+            return arena[:, at : at + count]
+
+        w1_round = [
+            take("w1", PACK * H).rearrange("p (t m j) -> p t m j", t=PACK, j=PACK),
+            held([P, PACK, P, PACK], BF16, "w1_round1")[:],
+        ]
         w1_codes = held([P, PASSES * H], U32, "w1_codes")
         w1_scale = held([P, PASSES * H], U8, "w1_scale")
 
@@ -206,23 +220,26 @@ def tile_list_land_air_exchange_kernel(
             nc.vector.quantize_mx(
                 w1_codes[:, a * H : (a + 1) * H].bitcast(E4M3),
                 w1_scale[:, a * H : (a + 1) * H],
-                w1_round[a][:].rearrange("p t m j -> p (t m j)"),
+                w1_round[a].rearrange("p t m j -> p (t m j)"),
             )
 
         raws = {"w4": w4_raw, "w5": w5_raw}
-        rounded = {name: held([P, N, PACK], BF16, name + "_round") for name in raws}
+        rounded = {
+            "w4": held([P, N, PACK], BF16, "w4_round")[:],
+            "w5": take("w5", PACK * N).rearrange("p (n t) -> p n t", t=PACK),
+        }
         second_codes = {name: held([P, N], U32, name + "_codes") for name in raws}
         second_scale = {name: held([P, N], U8, name + "_scale") for name in raws}
 
         def round_second(copy, name):
             copy(
-                rounded[name][:].rearrange("p (c i) t -> p c t i", i=4),
+                rounded[name].rearrange("p (c i) t -> p c t i", i=4),
                 raws[name][:].rearrange("p t (c i) -> p c t i", i=4),
             )
 
         def quantize_second(name):
             nc.vector.quantize_mx(
-                second_codes[name][:].bitcast(E4M3), second_scale[name][:], rounded[name][:].rearrange("p n t -> p (n t)")
+                second_codes[name][:].bitcast(E4M3), second_scale[name][:], rounded[name].rearrange("p n t -> p (n t)")
             )
 
         def first_weight(name, a, t):
@@ -242,8 +259,7 @@ def tile_list_land_air_exchange_kernel(
         names = ("h1", "h2", "h3")
         quantized = {}
         pairs = {}
-        stage = held([P, 3 * S * PACK], BF16, "stage")
-        stage_end = [0]
+        tanh_ring = ctx.enter_context(tc.tile_pool(name="tanh_ring", bufs=8))
         placed = {}
         chunked = set()
         words = {}
@@ -281,7 +297,7 @@ def tile_list_land_air_exchange_kernel(
         def tanh_quarter(name, quarter, halves=(0, 1), on=None):
             j0 = quarter * QUARTER
             if (name, quarter) not in pairs:
-                pairs[name, quarter] = held([P, 2, QUARTER, 2], F32, "%s_pairs%d" % (name, quarter), on)
+                pairs[name, quarter] = tanh_ring.tile([P, 2, QUARTER, 2], F32, name="pairs", align_bytes=64)
             for u in halves:
                 bank = first_banks.tile([P, 2, QUARTER], F32, name="first_bank")
                 for a in range(PASSES):
@@ -309,12 +325,7 @@ def tile_list_land_air_exchange_kernel(
             )
 
         def place(name, start, width, share, on=None):
-            if on is None:
-                at = stage_end[0] - PACK * share
-                stage_end[0] = at + PACK * width
-                placed[name, start] = stage[:, at : at + PACK * width]
-            else:
-                placed[name, start] = held([P, PACK * width], BF16, "%s_stage%d" % (name, start), on)[:]
+            placed[name, start] = take((name, start), PACK * width, PACK * share, on)
             if share:
                 apply_gain(nc.gpsimd, gain_columns[name], name, start, 0, share)
 
@@ -348,24 +359,30 @@ def tile_list_land_air_exchange_kernel(
                 )
             return bank
 
-        y2 = {q * QUARTER: held([P, HALVES, QUARTER], F32, "y2_%d" % q, 79872 + 2048 * q) for q in range(4)}
-        product = {q * QUARTER: held([P, HALVES, QUARTER], F32, "product%d" % q, 69632 + 2048 * q) for q in range(4)}
+        y2 = {
+            q * QUARTER: take("y%d" % q, 2 * HALVES * QUARTER).bitcast(F32).rearrange("p (u j) -> p u j", u=HALVES)
+            for q in range(4)
+        }
+        product = {
+            q * QUARTER: take("p%d" % q, 2 * HALVES * QUARTER).bitcast(F32).rearrange("p (u j) -> p u j", u=HALVES)
+            for q in range(4)
+        }
 
         def park_y2(start, width):
-            nc.scalar.copy(y2[start][:], second_stage("h2", start, width)[:])
+            nc.scalar.copy(y2[start], second_stage("h2", start, width)[:])
 
         def multiply(start, width):
             nc.vector.tensor_tensor(
-                product[start][:],
+                product[start],
                 second_stage("h1", start, width)[:],
-                y2[start][:],
+                y2[start],
                 MULT,
             )
 
         def finish(start, width):
             result = ring.tile([P, HALVES, width], F32, name="result")
             nc.vector.tensor_tensor(
-                result[:], second_stage("h3", start, width)[:], product[start][:], ADD
+                result[:], second_stage("h3", start, width)[:], product[start], ADD
             )
             nc.sync.dma_start(out.rearrange("(u p) j -> p u j", p=P)[:, :, start : start + width], result[:])
 
@@ -378,7 +395,7 @@ def tile_list_land_air_exchange_kernel(
         quantize_h("h2", 0, 256)
         tanh_quarter("h2", 1, (0,))
         tanh_quarter("h2", 1, (1,))
-        place("h2", 256, 512, 120, None)
+        place("h2", 256, 512, 120, ("h2", 0))
         own_gain("h2", 256, 120, 256)
         tanh_quarter("h2", 2, (0,))
         tanh_quarter("h2", 2, (1,))
@@ -390,7 +407,7 @@ def tile_list_land_air_exchange_kernel(
         round_w1(nc.scalar.copy, 0, 2, 3)
         round_w1(nc.vector.tensor_copy, 1, 0, 4)
         quantize_h("h2", 256, 512)
-        gain_piece("h2", 768, 256, 40, None)
+        gain_piece("h2", 768, 256, 40, ("h2", 256))
         round_w1(nc.scalar.copy, 0, 3, 4)
         quantize_w1(1)
         quantize_w1(0)
@@ -400,15 +417,15 @@ def tile_list_land_air_exchange_kernel(
         turn_gains()
         tanh_quarter("h3", 1, (0,))
         tanh_quarter("h3", 1, (1,))
-        place("h3", 0, 512, 120, None)
-        own_gain("h3", 0, 120, 256)
+        place("h3", 0, 512, 144, "w1")
+        own_gain("h3", 0, 144, 256)
         own_gain("h3", 0, 256, 512)
         tanh_quarter("h3", 2, (0,))
         tanh_quarter("h3", 2, (1,))
         round_second(nc.scalar.copy, "w5")
         quantize_second("w5")
         quantize_h("h3", 0, 512)
-        gain_piece("h3", 512, 256, 120, None)
+        gain_piece("h3", 512, 256, 136, "w5")
         tanh_quarter("h1", 0, (0,))
         tanh_quarter("h1", 0, (1,))
         round_second(nc.scalar.copy, "w4")
@@ -419,27 +436,25 @@ def tile_list_land_air_exchange_kernel(
         tanh_quarter("h1", 1, (0,))
         tanh_quarter("h1", 1, (1,))
         park_y2(0, 256)
-        gain_piece("h1", 256, 256, 80, None)
+        gain_piece("h1", 256, 256, 104, ("h3", 512))
         multiply(0, 256)
         quantize_h("h1", 256, 256)
         tanh_quarter("h1", 2, (0,))
         tanh_quarter("h1", 2, (1,))
         park_y2(256, 256)
-        gain_piece("h1", 512, 256, 152, 79872)
+        gain_piece("h1", 512, 256, 152, "y0")
         finish(0, 256)
         multiply(256, 256)
         quantize_h("h1", 512, 256)
-        tanh_quarter("h1", 3, (0,))
-        tanh_quarter("h1", 3, (1,))
-        park_y2(512, 256)
-        gain_piece("h1", 768, 256, 152, 81920)
+        tanh_quarter("h1", 3)
+        gain_piece("h1", 768, 256, 112, "y1")
         finish(256, 256)
-        multiply(512, 256)
         quantize_h("h1", 768, 256)
-        tanh_quarter("h3", 3, (0,))
-        tanh_quarter("h3", 3, (1,))
+        tanh_quarter("h3", 3)
+        park_y2(512, 256)
         park_y2(768, 256)
-        gain_piece("h3", 768, 256, 104, 83968)
+        gain_piece("h3", 768, 256, 152, "p1")
+        multiply(512, 256)
         multiply(768, 256)
         quantize_h("h3", 768, 256)
         finish(512, 256)

@@ -32,7 +32,7 @@ def tile_list_land_air_exchange_kernel(
     nc = tc.nc
     with ExitStack() as ctx:
         keep = ctx.enter_context(tc.tile_pool(name="keep", bufs=1))
-        ring = ctx.enter_context(tc.tile_pool(name="ring", bufs=4))
+        ring = ctx.enter_context(tc.tile_pool(name="ring", bufs=5))
         first_banks = ctx.enter_context(tc.psum_pool(name="first_banks", bufs=4))
         second_banks = ctx.enter_context(tc.psum_pool(name="second_banks", bufs=3))
         gain_banks = ctx.enter_context(tc.psum_pool(name="gain_banks", bufs=1))
@@ -188,11 +188,13 @@ def tile_list_land_air_exchange_kernel(
                 w3_codes[:].rearrange("p (a t b i) -> p a b t i", a=PASSES, t=PACK, i=4),
                 w3_raw[:].rearrange("p (a b i t) -> p a b t i", a=PASSES, t=PACK, i=4),
             )
+
+        def order_w3_scale():
             nc.vector.tensor_copy(
                 w3_scale[:].rearrange("p (t m) -> p t m", t=PACK), w3_scale_raw[:].rearrange("p (m t) -> p t m", t=PACK)
             )
 
-        arena = held([P, 37 * S], BF16, "arena")
+        arena = held([P, 42 * S], BF16, "arena")
         arena_end = [0]
         ends = {}
 
@@ -203,9 +205,10 @@ def tile_list_land_air_exchange_kernel(
                 arena_end[0] = at + count + 2 * PACK * QUARTER
             return arena[:, at : at + count]
 
+        w1_both = take("w1", PASSES * PACK * H)
         w1_round = [
-            take("w1", PACK * H).rearrange("p (t m j) -> p t m j", t=PACK, j=PACK),
-            held([P, PACK, P, PACK], BF16, "w1_round1")[:],
+            w1_both[:, a * PACK * H : (a + 1) * PACK * H].rearrange("p (t m j) -> p t m j", t=PACK, j=PACK)
+            for a in range(PASSES)
         ]
         w1_codes = held([P, PASSES * H], U32, "w1_codes")
         w1_scale = held([P, PASSES * H], U8, "w1_scale")
@@ -216,16 +219,12 @@ def tile_list_land_air_exchange_kernel(
                 w1_raw[a][:].rearrange("p j (e t i) -> p t e j i", t=PACK, i=4)[:, t0:t1],
             )
 
-        def quantize_w1(a):
-            nc.vector.quantize_mx(
-                w1_codes[:, a * H : (a + 1) * H].bitcast(E4M3),
-                w1_scale[:, a * H : (a + 1) * H],
-                w1_round[a].rearrange("p t m j -> p (t m j)"),
-            )
+        def quantize_w1():
+            nc.vector.quantize_mx(w1_codes[:].bitcast(E4M3), w1_scale[:], w1_both)
 
         raws = {"w4": w4_raw, "w5": w5_raw}
         rounded = {
-            "w4": held([P, N, PACK], BF16, "w4_round")[:],
+            "w4": take("w4", PACK * N).rearrange("p (n t) -> p n t", t=PACK),
             "w5": take("w5", PACK * N).rearrange("p (n t) -> p n t", t=PACK),
         }
         second_codes = {name: held([P, N], U32, name + "_codes") for name in raws}
@@ -259,7 +258,7 @@ def tile_list_land_air_exchange_kernel(
         names = ("h1", "h2", "h3")
         quantized = {}
         pairs = {}
-        tanh_ring = ctx.enter_context(tc.tile_pool(name="tanh_ring", bufs=8))
+        tanh_ring = ctx.enter_context(tc.tile_pool(name="tanh_ring", bufs=6))
         placed = {}
         chunked = set()
         words = {}
@@ -343,6 +342,14 @@ def tile_list_land_air_exchange_kernel(
             for c0 in range(0, width, P):
                 quantized[name, start + c0] = (codes, scale, c0)
 
+        def quantize_two(first, second):
+            at = ends[first] - PACK * QUARTER
+            codes = held([P, 2 * QUARTER], U32, "two_codes")
+            scale = held([P, 2 * QUARTER], U8, "two_scale")
+            nc.vector.quantize_mx(codes[:].bitcast(E4M3), scale[:], arena[:, at : at + 2 * PACK * QUARTER])
+            quantized[first] = (codes, scale, 0)
+            quantized[second] = (codes, scale, QUARTER)
+
         def second_stage(name, start, width):
             bank = second_banks.tile([P, HALVES, width], F32, name="second_bank")
             h_codes, h_scale, c0 = quantized[name, start]
@@ -379,12 +386,13 @@ def tile_list_land_air_exchange_kernel(
                 MULT,
             )
 
-        def finish(start, width):
-            result = ring.tile([P, HALVES, width], F32, name="result")
-            nc.vector.tensor_tensor(
-                result[:], second_stage("h3", start, width)[:], product[start], ADD
-            )
-            nc.sync.dma_start(out.rearrange("(u p) j -> p u j", p=P)[:, :, start : start + width], result[:])
+        def finish(start, width, apart=False):
+            bank = second_stage("h3", start, width)
+            rows = out.rearrange("(u p) j -> p u j", p=P)[:, :, start : start + width]
+            for u0, u1 in ((0, 1), (1, 2)) if apart else ((0, 2),):
+                result = ring.tile([P, u1 - u0, width], F32, name="result")
+                nc.vector.tensor_tensor(result[:], bank[:, u0:u1], product[start][:, u0:u1], ADD)
+                nc.sync.dma_start(rows[:, u0:u1], result[:])
 
         tanh_chunk("h2", 0)
         place("h2", 0, 256, 0, None)
@@ -392,6 +400,7 @@ def tile_list_land_air_exchange_kernel(
         tanh_chunk("h2", 128)
         own_gain("h2", 0, 128, 256)
         order_w3()
+        order_w3_scale()
         quantize_h("h2", 0, 256)
         tanh_quarter("h2", 1, (0,))
         tanh_quarter("h2", 1, (1,))
@@ -409,8 +418,7 @@ def tile_list_land_air_exchange_kernel(
         quantize_h("h2", 256, 512)
         gain_piece("h2", 768, 256, 40, ("h2", 256))
         round_w1(nc.scalar.copy, 0, 3, 4)
-        quantize_w1(1)
-        quantize_w1(0)
+        quantize_w1()
         quantize_h("h2", 768, 256)
         tanh_quarter("h3", 0, (0,))
         tanh_quarter("h3", 0, (1,))
@@ -429,14 +437,13 @@ def tile_list_land_air_exchange_kernel(
         tanh_quarter("h1", 0, (0,))
         tanh_quarter("h1", 0, (1,))
         round_second(nc.scalar.copy, "w4")
-        gain_piece("h1", 0, 256, 0, None)
+        gain_piece("h1", 0, 256, 0, ("h3", 512))
         quantize_second("w4")
-        quantize_h("h3", 512, 256)
-        quantize_h("h1", 0, 256)
+        quantize_two(("h3", 512), ("h1", 0))
         tanh_quarter("h1", 1, (0,))
         tanh_quarter("h1", 1, (1,))
         park_y2(0, 256)
-        gain_piece("h1", 256, 256, 104, ("h3", 512))
+        gain_piece("h1", 256, 256, 104, "w4")
         multiply(0, 256)
         quantize_h("h1", 256, 256)
         tanh_quarter("h1", 2, (0,))
@@ -458,4 +465,4 @@ def tile_list_land_air_exchange_kernel(
         multiply(768, 256)
         quantize_h("h3", 768, 256)
         finish(512, 256)
-        finish(768, 256)
+        finish(768, 256, True)

@@ -179,9 +179,9 @@ def tile_list_land_air_exchange_kernel(
                 w6_scale[32 * d : 32 * d + 4, :].bitcast(I32), w6_scales[0, 4 * d : 4 * d + 4, :].bitcast(I32)
             )
 
-        first_pairs = held([P, 2 * QUARTER * 2], F32, "first_pairs", 0)
+        first_chunks = [held([P, P * PACK], F32, "first_chunk%d" % c, (2048, 57344)[c]) for c in range(2)]
         w3_codes = held([P, PASSES * H], I32, "w3_codes", 0)
-        w3_scale = held([P, H], U8, "w3_scale", 4096)
+        w3_scale = held([P, H], U8, "w3_scale", 57344)
 
         def order_w3():
             nc.vector.tensor_copy(
@@ -206,8 +206,9 @@ def tile_list_land_air_exchange_kernel(
             return arena[:, at : at + count]
 
         w1_both = take("w1", PASSES * PACK * H)
+        arena_end[0] = arena_end[0] + 2 * PACK * QUARTER
         w1_round = [
-            w1_both[:, a * PACK * H : (a + 1) * PACK * H].rearrange("p (t m j) -> p t m j", t=PACK, j=PACK)
+            w1_both[:, (1 - a) * PACK * H : (2 - a) * PACK * H].rearrange("p (t m j) -> p t m j", t=PACK, j=PACK)
             for a in range(PASSES)
         ]
         w1_codes = held([P, PASSES * H], U32, "w1_codes")
@@ -244,6 +245,7 @@ def tile_list_land_air_exchange_kernel(
         def first_weight(name, a, t):
             c0 = a * H + t * P
             if name == "h1":
+                c0 = (1 - a) * H + t * P
                 return w1_codes[:, c0 : c0 + P].bitcast(E4M3), w1_scale[:, c0 : c0 + P]
             if name == "h2":
                 return w2_codes[:, 2 * c0 : 2 * (c0 + P)].bitcast(E2M1), w2_scale[:, c0 : c0 + P]
@@ -265,7 +267,7 @@ def tile_list_land_air_exchange_kernel(
 
         def tanh_view(name, j0, j1):
             if name == "h2" and j1 <= QUARTER:
-                return first_pairs[:].rearrange("p (j u e) -> p u j e", u=2, e=2)[:, :, j0:j1]
+                return first_chunks[j0 // P][:].rearrange("p (j u e) -> p u j e", u=2, e=2)
             if (name, j0 // QUARTER) in chunked:
                 return words[name][:].rearrange("p (j u e) -> p u j e", u=2, e=2)[:, :, j0:j1]
             q = j0 // QUARTER
@@ -274,7 +276,7 @@ def tile_list_land_air_exchange_kernel(
         def tanh_chunk(name, j0):
             bank = first_banks.tile([P, PACK, P], F32, name="first_bank")
             chunked.add((name, j0 // QUARTER))
-            tile = first_pairs
+            tile = first_chunks[j0 // P]
             for a in range(PASSES):
                 for t in range(PACK):
                     codes, scale = first_weight(name, a, t)
@@ -288,7 +290,7 @@ def tile_list_land_air_exchange_kernel(
                         stop=(a == PASSES - 1 and t == PACK - 1),
                     )
             nc.scalar.activation(
-                tile[:, PACK * j0 : PACK * (j0 + P)].rearrange("p (j t) -> p j t", t=PACK),
+                tile[:].rearrange("p (j t) -> p j t", t=PACK),
                 bank[:].rearrange("p t j -> p j t"),
                 TANH,
             )
@@ -324,7 +326,7 @@ def tile_list_land_air_exchange_kernel(
             )
 
         def place(name, start, width, share, on=None):
-            placed[name, start] = take((name, start), PACK * width, PACK * share, on)
+            placed[name, start] = take((name, start), PACK * width, PACK * (8 if on == "w1" and not share else share), on)
             if share:
                 apply_gain(nc.gpsimd, gain_columns[name], name, start, 0, share)
 
@@ -395,17 +397,18 @@ def tile_list_land_air_exchange_kernel(
                 nc.sync.dma_start(rows[:, u0:u1], result[:])
 
         tanh_chunk("h2", 0)
-        place("h2", 0, 256, 0, None)
+        place("h2", 0, 256, 0, "w1")
         own_gain("h2", 0, 0, 128)
         tanh_chunk("h2", 128)
         own_gain("h2", 0, 128, 256)
         order_w3()
-        order_w3_scale()
         quantize_h("h2", 0, 256)
+        order_w3_scale()
+        round_w1(nc.vector.tensor_copy, 0, 3, 4)
         tanh_quarter("h2", 1, (0,))
         tanh_quarter("h2", 1, (1,))
-        place("h2", 256, 512, 120, ("h2", 0))
-        own_gain("h2", 256, 120, 256)
+        place("h2", 256, 512, 144, ("h2", 0))
+        own_gain("h2", 256, 144, 256)
         tanh_quarter("h2", 2, (0,))
         tanh_quarter("h2", 2, (1,))
         own_gain("h2", 256, 256, 512)
@@ -417,7 +420,6 @@ def tile_list_land_air_exchange_kernel(
         round_w1(nc.vector.tensor_copy, 1, 0, 4)
         quantize_h("h2", 256, 512)
         gain_piece("h2", 768, 256, 40, ("h2", 256))
-        round_w1(nc.scalar.copy, 0, 3, 4)
         quantize_w1()
         quantize_h("h2", 768, 256)
         tanh_quarter("h3", 0, (0,))
@@ -425,15 +427,15 @@ def tile_list_land_air_exchange_kernel(
         turn_gains()
         tanh_quarter("h3", 1, (0,))
         tanh_quarter("h3", 1, (1,))
-        place("h3", 0, 512, 144, "w1")
-        own_gain("h3", 0, 144, 256)
+        place("h3", 0, 512, 160, "w1")
+        own_gain("h3", 0, 160, 256)
         own_gain("h3", 0, 256, 512)
         tanh_quarter("h3", 2, (0,))
         tanh_quarter("h3", 2, (1,))
         round_second(nc.scalar.copy, "w5")
         quantize_second("w5")
         quantize_h("h3", 0, 512)
-        gain_piece("h3", 512, 256, 136, "w5")
+        gain_piece("h3", 512, 256, 152, "w5")
         tanh_quarter("h1", 0, (0,))
         tanh_quarter("h1", 0, (1,))
         round_second(nc.scalar.copy, "w4")
@@ -443,24 +445,24 @@ def tile_list_land_air_exchange_kernel(
         tanh_quarter("h1", 1, (0,))
         tanh_quarter("h1", 1, (1,))
         park_y2(0, 256)
-        gain_piece("h1", 256, 256, 104, "w4")
+        gain_piece("h1", 256, 256, 96, "w4")
         multiply(0, 256)
         quantize_h("h1", 256, 256)
         tanh_quarter("h1", 2, (0,))
         tanh_quarter("h1", 2, (1,))
         park_y2(256, 256)
-        gain_piece("h1", 512, 256, 152, "y0")
+        gain_piece("h1", 512, 256, 144, "y0")
         finish(0, 256)
         multiply(256, 256)
         quantize_h("h1", 512, 256)
         tanh_quarter("h1", 3)
-        gain_piece("h1", 768, 256, 112, "y1")
+        gain_piece("h1", 768, 256, 96, "y1")
         finish(256, 256)
         quantize_h("h1", 768, 256)
         tanh_quarter("h3", 3)
         park_y2(512, 256)
         park_y2(768, 256)
-        gain_piece("h3", 768, 256, 152, "p1")
+        gain_piece("h3", 768, 256, 144, "p1")
         multiply(512, 256)
         multiply(768, 256)
         quantize_h("h3", 768, 256)

@@ -168,9 +168,9 @@ def tile_list_land_air_exchange_kernel(
             nc.sync.dma_start(w1_raw[a][:], w1_rows[a])
         nc.sync.dma_start(gain_rows[0:1, :], gain3.unsqueeze(0))
         nc.sync.dma_start(
-            gain_rows[4:8, 0:P].rearrange("t (b i) -> t b i", i=4), gain1.rearrange("(b t i) -> t b i", t=PACK, i=4)
+            gain_rows[4:8, 0:P].rearrange("t (b i) -> t b i", i=8), gain1.rearrange("(b t i) -> t b i", t=PACK, i=8)
         )
-        for raw, w, run in ((w5_raw, w5, 8), (w4_raw, w4, 4)):
+        for raw, w, run in ((w5_raw, w5, 8), (w4_raw, w4, 8)):
             for t in range(PACK):
                 nc.sync.dma_start(raw[:, t, :], w.rearrange("(b t i) n -> t b i n", t=PACK, i=run)[t])
         nc.sync.dma_start(w6_codes[:].bitcast(I32), w6_words[0].bitcast(I32))
@@ -185,13 +185,14 @@ def tile_list_land_air_exchange_kernel(
 
         def order_w3():
             nc.vector.tensor_copy(
-                w3_codes[:].rearrange("p (a t b i) -> p a b t i", a=PASSES, t=PACK, i=4),
-                w3_raw[:].rearrange("p (a b i t) -> p a b t i", a=PASSES, t=PACK, i=4),
+                w3_codes[:].rearrange("p (a t m) -> p a m t", a=PASSES, t=PACK),
+                w3_raw[:].rearrange("p (a m t) -> p a m t", a=PASSES, t=PACK),
             )
 
         def order_w3_scale():
             nc.vector.tensor_copy(
-                w3_scale[:].rearrange("p (t m) -> p t m", t=PACK), w3_scale_raw[:].rearrange("p (m t) -> p t m", t=PACK)
+                w3_scale[:].rearrange("p (t b i) -> p b t i", t=PACK, i=16),
+                w3_scale_raw[:].rearrange("p (b i t) -> p b t i", t=PACK, i=16),
             )
 
         arena = held([P, 42 * S], BF16, "arena")
@@ -216,8 +217,8 @@ def tile_list_land_air_exchange_kernel(
 
         def round_w1(copy, a, t0, t1):
             copy(
-                w1_round[a][:, t0:t1].rearrange("p t (e i) j -> p t e j i", i=4),
-                w1_raw[a][:].rearrange("p j (e t i) -> p t e j i", t=PACK, i=4)[:, t0:t1],
+                w1_round[a][:, t0:t1].rearrange("p t (e i) j -> p t e j i", i=8),
+                w1_raw[a][:].rearrange("p j (e t i) -> p t e j i", t=PACK, i=8)[:, t0:t1],
             )
 
         def quantize_w1():

from contextlib import ExitStack

import concourse.mybir as mybir
from concourse.masks import make_identity

K, H, N, T, S = 1024, 512, 256, 2048, 1024
FLOPS = 2 * 3 * S * (K * H + H * N)

F32 = mybir.dt.float32
BF16 = mybir.dt.bfloat16
I32 = mybir.dt.int32
U32 = mybir.dt.uint32
U16 = mybir.dt.uint16
U8 = mybir.dt.uint8
E4M3 = mybir.dt.float8_e4m3fn_x4
E2M1 = mybir.dt.float4_e2m1fn_x4
TANH = mybir.ActivationFunctionType.Tanh
MULT = mybir.AluOpType.mult
ADD = mybir.AluOpType.add

P = 128
PACK = 4
PASSES = K // (P * PACK)
QUARTER = 256
HALVES = N // P


def tile_list_land_air_exchange_kernel(
    tc, tab_words, tab_scales, offs, w1, w2_words, w2_scales, w3_words, w3_scales,
    gain1, gain2, gain3, w4, w5, w6_words, w6_scales, out,
):
    nc = tc.nc
    with ExitStack() as ctx:
        keep = ctx.enter_context(tc.tile_pool(name="keep", bufs=1))
        ring = ctx.enter_context(tc.tile_pool(name="ring", bufs=5))
        first_banks = ctx.enter_context(tc.psum_pool(name="first_banks", bufs=4))
        second_banks = ctx.enter_context(tc.psum_pool(name="second_banks", bufs=3))
        gain_banks = ctx.enter_context(tc.psum_pool(name="gain_banks", bufs=1))
        shared = ctx.enter_context(tc.tile_pool(name="shared", bufs=1))

        def held(shape, dtype, name, at=None):
            if at is None:
                return keep.tile(shape, dtype, name=name, align_bytes=64)
            return shared.tile(shape, dtype, name=name, align_bytes=64, offset=at)

        offsets = keep.tile([P, S // 16], U16, name="offsets")
        nc.sync.dma_start(offsets[:], offs)

        scale_window = held([P, T], U8, "scale_window")
        word_window = [held([P, T], U32, "word_window%d" % a, (45696, 18304)[a]) for a in range(PASSES)]
        w2_raw = held([P, PASSES * H * 2], U8, "w2_raw", 8128)
        w2_scale_raw = held([P, PASSES * H], U8, "w2_scale_raw")
        w3_scale_raw = held([P, H], U8, "w3_scale_raw")
        w6_scale = held([P, N], U8, "w6_scale")
        gain_rows = held([P, H], F32, "gain_rows")
        gain2_rows = held([P, P], F32, "gain2_rows")
        identity = held([P, P], F32, "identity")
        v_scale = held([P, PASSES * S], U8, "v_scale")
        nc.gpsimd.memset(w2_scale_raw[:].bitcast(I32), 0)
        nc.gpsimd.memset(gain2_rows[:], 0.0)
        nc.gpsimd.memset(w3_scale_raw[:].bitcast(I32), 0)
        nc.vector.memset(v_scale[:, S:].bitcast(I32), 0)

        def load_w2_scale(d):
            nc.sync.dma_start(
                w2_scale_raw[32 * d : 32 * d + 4, :].bitcast(I32).rearrange("p (a c) -> p a c", a=PASSES),
                w2_scales[:, 4 * d : 4 * d + 4, :].bitcast(I32).rearrange("a r c -> r a c"),
            )

        def load_words(a):
            nc.sync.dma_start(word_window[a][:].bitcast(I32), tab_words[a].rearrange("p t i -> p (t i)").bitcast(I32))

        for a in range(PASSES):
            nc.sync.dma_start(
                scale_window[a:P:PASSES, :].bitcast(I32),
                tab_scales[a].bitcast(I32).unsqueeze(1).to_broadcast([16, 4, T // 4]),
            )
        nc.sync.dma_start(
            w2_raw[:].bitcast(I32).rearrange("p (a c) -> p a c", a=PASSES),
            w2_words.bitcast(I32).rearrange("a p c -> p a c"),
        )
        for d in range(3):
            load_w2_scale(d)
        load_words(0)
        load_w2_scale(3)
        nc.sync.dma_start(
            gain2_rows[0:PACK, :].rearrange("t (b i) -> t b i", i=8), gain2.rearrange("(b t i) -> t b i", t=PACK, i=8)
        )
        for d in range(4):
            nc.sync.dma_start(
                w3_scale_raw[32 * d : 32 * d + 4 * PASSES, :].bitcast(I32),
                w3_scales[:, 4 * d : 4 * d + 4, :].bitcast(I32),
            )
        load_words(1)
        make_identity(nc, identity[:])
        nc.gpsimd.memset(gain_rows[:], 0.0)
        nc.gpsimd.memset(w6_scale[:].bitcast(I32), 0)

        gain2_bank = second_banks.tile([P, P], F32, name="second_bank")
        nc.tensor.transpose(gain2_bank[:], gain2_rows[:], identity[:])
        gain_bank = gain_banks.tile([P, PACK + P], F32, name="gain_bank")
        gain_at = {"h3": 0, "h1": 8}
        gains = {name: gain_bank[:, at : at + PACK] for name, at in gain_at.items()}
        gains["h2"] = gain2_bank[:, 0:PACK]
        gain_copy = held([P, 12], F32, "gain_copy")
        gain2_copy = held([P, PACK], F32, "gain2_copy", 18304)
        gain_columns = {name: gain_copy[:, at : at + PACK] for name, at in gain_at.items()}
        gain_columns["h2"] = gain2_copy[:]

        def turn_gains():
            for t in range(PACK):
                nc.tensor.transpose(gain_bank[:, t : t + P], gain_rows[:, t:H:PACK], identity[:])
            nc.tensor.transpose(gain_bank[:, PACK : PACK + P], gain_rows[:, 0:P], identity[:])
            nc.scalar.copy(gain_copy[:], gain_bank[:, 0:12])

        picked_scale = held([P, S], U8, "picked_scale", 34624)
        nc.vector.tensor_copy(picked_scale[:], scale_window[:].indirect(offsets[:]))
        nc.vector.tensor_copy(v_scale[:, 0:S].bitcast(I32), picked_scale[:].bitcast(I32))
        for a, r in [(1, 0), (1, 1), (1, 2), (1, 3), (0, 1), (0, 2), (0, 3)]:
            nc.sync.dma_start(
                v_scale[r:P:32, a * S : (a + 1) * S].bitcast(I32),
                picked_scale[8 * r + a : P : 32, :].bitcast(I32),
            )
        v_codes = [held([P, S], U32, "v_codes%d" % a) for a in range(PASSES)]

        def gather_words(a, j0, j1):
            nc.vector.tensor_copy(v_codes[a][:, j0:j1], word_window[a][:].indirect(offsets[:, j0 // 16 : j1 // 16]))

        w2_codes = held([P, PASSES * H * 2], U8, "w2_codes")
        w2_scale = held([P, PASSES * H], U8, "w2_scale")
        nc.vector.tensor_copy(
            w2_codes[:].bitcast(I32).rearrange("p (a t b w) -> p a t b w", a=PASSES, t=PACK, w=4),
            w2_raw[:].bitcast(I32).rearrange("p (a b t w) -> p a t b w", a=PASSES, t=PACK, w=4),
        )
        gather_words(0, 0, QUARTER)
        warm_bank = first_banks.tile([P, 2, QUARTER], F32, name="first_bank")
        for n in range(6):
            nc.tensor.matmul_mx(
                warm_bank[:, n % 2, :],
                lhsT=v_codes[0][:, 0:P].bitcast(E4M3),
                lhsT_scale=picked_scale[:, 0:P],
                rhs=v_codes[0][:, 0:QUARTER].bitcast(E4M3),
                rhs_scale=picked_scale[:, 0:QUARTER],
                start=(n == 0),
                stop=(n == 5),
            )
        gather_words(0, QUARTER, S)
        nc.vector.tensor_copy(
            w2_scale[:].bitcast(I32).rearrange("p (a t b w) -> p a t b w", a=PASSES, t=PACK, w=2),
            w2_scale_raw[:].bitcast(I32).rearrange("p (a b t w) -> p a t b w", a=PASSES, t=PACK, w=2),
        )
        gather_words(1, 0, QUARTER)
        gather_words(1, QUARTER, 2 * QUARTER)
        gather_words(1, 2 * QUARTER, S)
        nc.vector.tensor_copy(gain2_copy[:], gains["h2"])

        w1_raw = [held([P, PACK, H], F32, "w1_raw%d" % a, (10112, 45696)[a]) for a in range(PASSES)]
        w3_raw = held([P, PASSES * H], I32, "w3_raw", 4096)
        w6_codes = held([P, 2 * N], U8, "w6_codes", 34944)
        w5_raw = held([P, PACK, N], F32, "w5_raw", 35584)
        w4_raw = held([P, PACK, N], F32, "w4_raw", 30592)
        w1_rows = w1.rearrange("(a p j) r -> a p j r", a=PASSES, j=PACK)
        nc.gpsimd.dma_start(
            w3_raw[:].rearrange("p (a c) -> p a c", a=PASSES),
            w3_words.rearrange("a p c i -> p a (c i)").bitcast(I32),
        )
        for a in range(PASSES):
            nc.sync.dma_start(w1_raw[a][:], w1_rows[a])
        nc.sync.dma_start(gain_rows[0:1, :], gain3.unsqueeze(0))
        nc.sync.dma_start(
            gain_rows[4:8, 0:P].rearrange("t (b i) -> t b i", i=8), gain1.rearrange("(b t i) -> t b i", t=PACK, i=8)
        )
        for raw, w, run in ((w5_raw, w5, 8), (w4_raw, w4, 8)):
            for t in range(PACK):
                nc.sync.dma_start(raw[:, t, :], w.rearrange("(b t i) n -> t b i n", t=PACK, i=run)[t])
        nc.sync.dma_start(w6_codes[:].bitcast(I32), w6_words[0].bitcast(I32))
        for d in range(4):
            nc.sync.dma_start(
                w6_scale[32 * d : 32 * d + 4, :].bitcast(I32), w6_scales[0, 4 * d : 4 * d + 4, :].bitcast(I32)
            )

        first_chunks = [held([P, P * PACK], F32, "first_chunk%d" % c, (2048, 57344)[c]) for c in range(2)]
        w3_codes = held([P, PASSES * H], I32, "w3_codes", 0)
        w3_scale = held([P, H], U8, "w3_scale", 57344)

        def order_w3():
            nc.vector.tensor_copy(
                w3_codes[:].rearrange("p (a t m) -> p a m t", a=PASSES, t=PACK),
                w3_raw[:].rearrange("p (a m t) -> p a m t", a=PASSES, t=PACK),
            )

        def order_w3_scale():
            nc.vector.tensor_copy(
                w3_scale[:].rearrange("p (t b i) -> p b t i", t=PACK, i=16),
                w3_scale_raw[:].rearrange("p (b i t) -> p b t i", t=PACK, i=16),
            )

        arena = held([P, 42 * S], BF16, "arena")
        arena_end = [0]
        ends = {}

        def take(key, count, back=0, behind=None):
            at = (arena_end[0] if behind is None else ends[behind]) - back
            ends[key] = at + count
            if behind is None:
                arena_end[0] = at + count + 2 * PACK * QUARTER
            return arena[:, at : at + count]

        w1_both = take("w1", PASSES * PACK * H)
        arena_end[0] = arena_end[0] + 2 * PACK * QUARTER
        w1_round = [
            w1_both[:, (1 - a) * PACK * H : (2 - a) * PACK * H].rearrange("p (t m j) -> p t m j", t=PACK, j=PACK)
            for a in range(PASSES)
        ]
        w1_codes = held([P, PASSES * H], U32, "w1_codes")
        w1_scale = held([P, PASSES * H], U8, "w1_scale")

        def round_w1(copy, a, t0, t1):
            copy(
                w1_round[a][:, t0:t1].rearrange("p t (e i) j -> p t e j i", i=8),
                w1_raw[a][:].rearrange("p j (e t i) -> p t e j i", t=PACK, i=8)[:, t0:t1],
            )

        def quantize_w1():
            nc.vector.quantize_mx(w1_codes[:].bitcast(E4M3), w1_scale[:], w1_both)

        raws = {"w4": w4_raw, "w5": w5_raw}
        rounded = {
            "w4": take("w4", PACK * N).rearrange("p (n t) -> p n t", t=PACK),
            "w5": take("w5", PACK * N).rearrange("p (n t) -> p n t", t=PACK),
        }
        second_codes = {name: held([P, N], U32, name + "_codes") for name in raws}
        second_scale = {name: held([P, N], U8, name + "_scale") for name in raws}

        def round_second(copy, name):
            copy(
                rounded[name].rearrange("p (c i) t -> p c t i", i=4),
                raws[name][:].rearrange("p t (c i) -> p c t i", i=4),
            )

        def quantize_second(name):
            nc.vector.quantize_mx(
                second_codes[name][:].bitcast(E4M3), second_scale[name][:], rounded[name].rearrange("p n t -> p (n t)")
            )

        def first_weight(name, a, t):
            c0 = a * H + t * P
            if name == "h1":
                c0 = (1 - a) * H + t * P
                return w1_codes[:, c0 : c0 + P].bitcast(E4M3), w1_scale[:, c0 : c0 + P]
            if name == "h2":
                return w2_codes[:, 2 * c0 : 2 * (c0 + P)].bitcast(E2M1), w2_scale[:, c0 : c0 + P]
            return w3_codes[:, c0 : c0 + P].bitcast(E4M3), w3_scale[4 * a : P, t * P : (t + 1) * P]

        def second_weight(name, u):
            if name == "h3":
                return w6_codes[:, 2 * u * P : 2 * (u + 1) * P].bitcast(E2M1), w6_scale[:, u * P : (u + 1) * P]
            w = "w4" if name == "h1" else "w5"
            return second_codes[w][:, u * P : (u + 1) * P].bitcast(E4M3), second_scale[w][:, u * P : (u + 1) * P]

        names = ("h1", "h2", "h3")
        quantized = {}
        pairs = {}
        tanh_ring = ctx.enter_context(tc.tile_pool(name="tanh_ring", bufs=6))
        placed = {}
        chunked = set()
        words = {}

        def tanh_view(name, j0, j1):
            if name == "h2" and j1 <= QUARTER:
                return first_chunks[j0 // P][:].rearrange("p (j u e) -> p u j e", u=2, e=2)
            if (name, j0 // QUARTER) in chunked:
                return words[name][:].rearrange("p (j u e) -> p u j e", u=2, e=2)[:, :, j0:j1]
            q = j0 // QUARTER
            return pairs[name, q][:, :, j0 - q * QUARTER : j1 - q * QUARTER]

        def tanh_chunk(name, j0):
            bank = first_banks.tile([P, PACK, P], F32, name="first_bank")
            chunked.add((name, j0 // QUARTER))
            tile = first_chunks[j0 // P]
            for a in range(PASSES):
                for t in range(PACK):
                    codes, scale = first_weight(name, a, t)
                    nc.tensor.matmul_mx(
                        bank[:, t, :],
                        lhsT=codes,
                        lhsT_scale=scale,
                        rhs=v_codes[a][:, j0 : j0 + P].bitcast(E4M3),
                        rhs_scale=v_scale[:, a * S + j0 : a * S + j0 + P],
                        start=(a == 0 and t == 0),
                        stop=(a == PASSES - 1 and t == PACK - 1),
                    )
            nc.scalar.activation(
                tile[:].rearrange("p (j t) -> p j t", t=PACK),
                bank[:].rearrange("p t j -> p j t"),
                TANH,
            )

        def tanh_quarter(name, quarter, halves=(0, 1), on=None):
            j0 = quarter * QUARTER
            if (name, quarter) not in pairs:
                pairs[name, quarter] = tanh_ring.tile([P, 2, QUARTER, 2], F32, name="pairs", align_bytes=64)
            for u in halves:
                bank = first_banks.tile([P, 2, QUARTER], F32, name="first_bank")
                for a in range(PASSES):
                    for e in range(2):
                        codes, scale = first_weight(name, a, 2 * u + e)
                        nc.tensor.matmul_mx(
                            bank[:, e, :],
                            lhsT=codes,
                            lhsT_scale=scale,
                            rhs=v_codes[a][:, j0 : j0 + QUARTER].bitcast(E4M3),
                            rhs_scale=v_scale[:, a * S + j0 : a * S + j0 + QUARTER],
                            start=(a == 0 and e == 0),
                            stop=(a == PASSES - 1 and e == 1),
                        )
                nc.scalar.activation(
                    tanh_view(name, j0, j0 + QUARTER)[:, u], bank[:].rearrange("p e j -> p j e"), TANH
                )

        def apply_gain(engine, gain, name, start, c0, c1):
            engine.tensor_tensor(
                placed[name, start][:, PACK * c0 : PACK * c1].rearrange("p (j u e) -> p j u e", u=2, e=2),
                tanh_view(name, start + c0, start + c1).rearrange("p u j e -> p j u e"),
                gain.rearrange("p (u e) -> p u e", e=2).unsqueeze(1).to_broadcast([P, c1 - c0, 2, 2]),
                MULT,
            )

        def place(name, start, width, share, on=None):
            placed[name, start] = take((name, start), PACK * width, PACK * (8 if on == "w1" and not share else share), on)
            if share:
                apply_gain(nc.gpsimd, gain_columns[name], name, start, 0, share)

        def own_gain(name, start, c0, c1):
            apply_gain(nc.vector, gains[name], name, start, c0, c1)

        def gain_piece(name, start, width, share, on=None):
            place(name, start, width, share, on)
            own_gain(name, start, share, width)

        def quantize_h(name, start, width, on=None):
            codes = held([P, width], U32, "%s_codes%d" % (name, start), on)
            scale = held([P, width], U8, "%s_scale%d" % (name, start))
            nc.vector.quantize_mx(codes[:].bitcast(E4M3), scale[:], placed[name, start])
            for c0 in range(0, width, P):
                quantized[name, start + c0] = (codes, scale, c0)

        def quantize_two(first, second):
            at = ends[first] - PACK * QUARTER
            codes = held([P, 2 * QUARTER], U32, "two_codes")
            scale = held([P, 2 * QUARTER], U8, "two_scale")
            nc.vector.quantize_mx(codes[:].bitcast(E4M3), scale[:], arena[:, at : at + 2 * PACK * QUARTER])
            quantized[first] = (codes, scale, 0)
            quantized[second] = (codes, scale, QUARTER)

        def second_stage(name, start, width):
            bank = second_banks.tile([P, HALVES, width], F32, name="second_bank")
            h_codes, h_scale, c0 = quantized[name, start]
            for u in range(HALVES):
                codes, scale = second_weight(name, u)
                nc.tensor.matmul_mx(
                    bank[:, u, :],
                    lhsT=codes,
                    lhsT_scale=scale,
                    rhs=h_codes[:, c0 : c0 + width].bitcast(E4M3),
                    rhs_scale=h_scale[:, c0 : c0 + width],
                    start=True,
                    stop=True,
                )
            return bank

        y2 = {
            q * QUARTER: take("y%d" % q, 2 * HALVES * QUARTER).bitcast(F32).rearrange("p (u j) -> p u j", u=HALVES)
            for q in range(4)
        }
        product = {
            q * QUARTER: take("p%d" % q, 2 * HALVES * QUARTER).bitcast(F32).rearrange("p (u j) -> p u j", u=HALVES)
            for q in range(4)
        }

        def park_y2(start, width):
            nc.scalar.copy(y2[start], second_stage("h2", start, width)[:])

        def multiply(start, width):
            nc.vector.tensor_tensor(
                product[start],
                second_stage("h1", start, width)[:],
                y2[start],
                MULT,
            )

        def finish(start, width, apart=False):
            bank = second_stage("h3", start, width)
            rows = out.rearrange("(u p) j -> p u j", p=P)[:, :, start : start + width]
            for u0, u1 in ((0, 1), (1, 2)) if apart else ((0, 2),):
                result = ring.tile([P, u1 - u0, width], F32, name="result")
                nc.vector.tensor_tensor(result[:], bank[:, u0:u1], product[start][:, u0:u1], ADD)
                nc.sync.dma_start(rows[:, u0:u1], result[:])

        tanh_chunk("h2", 0)
        place("h2", 0, 256, 0, "w1")
        own_gain("h2", 0, 0, 128)
        tanh_chunk("h2", 128)
        own_gain("h2", 0, 128, 256)
        order_w3()
        quantize_h("h2", 0, 256)
        order_w3_scale()
        round_w1(nc.vector.tensor_copy, 0, 3, 4)
        tanh_quarter("h2", 1, (0,))
        tanh_quarter("h2", 1, (1,))
        place("h2", 256, 512, 144, ("h2", 0))
        own_gain("h2", 256, 144, 256)
        tanh_quarter("h2", 2, (0,))
        tanh_quarter("h2", 2, (1,))
        own_gain("h2", 256, 256, 512)
        round_w1(nc.scalar.copy, 0, 0, 1)
        tanh_quarter("h2", 3, (0,))
        round_w1(nc.scalar.copy, 0, 1, 2)
        tanh_quarter("h2", 3, (1,))
        round_w1(nc.scalar.copy, 0, 2, 3)
        round_w1(nc.vector.tensor_copy, 1, 0, 4)
        quantize_h("h2", 256, 512)
        gain_piece("h2", 768, 256, 40, ("h2", 256))
        quantize_w1()
        quantize_h("h2", 768, 256)
        tanh_quarter("h3", 0, (0,))
        tanh_quarter("h3", 0, (1,))
        turn_gains()
        tanh_quarter("h3", 1, (0,))
        tanh_quarter("h3", 1, (1,))
        place("h3", 0, 512, 160, "w1")
        own_gain("h3", 0, 160, 256)
        own_gain("h3", 0, 256, 512)
        tanh_quarter("h3", 2, (0,))
        tanh_quarter("h3", 2, (1,))
        round_second(nc.scalar.copy, "w5")
        quantize_second("w5")
        quantize_h("h3", 0, 512)
        gain_piece("h3", 512, 256, 152, "w5")
        tanh_quarter("h1", 0, (0,))
        tanh_quarter("h1", 0, (1,))
        round_second(nc.scalar.copy, "w4")
        gain_piece("h1", 0, 256, 0, ("h3", 512))
        quantize_second("w4")
        quantize_two(("h3", 512), ("h1", 0))
        tanh_quarter("h1", 1, (0,))
        tanh_quarter("h1", 1, (1,))
        park_y2(0, 256)
        gain_piece("h1", 256, 256, 96, "w4")
        multiply(0, 256)
        quantize_h("h1", 256, 256)
        tanh_quarter("h1", 2, (0,))
        tanh_quarter("h1", 2, (1,))
        park_y2(256, 256)
        gain_piece("h1", 512, 256, 144, "y0")
        finish(0, 256)
        multiply(256, 256)
        quantize_h("h1", 512, 256)
        tanh_quarter("h1", 3)
        gain_piece("h1", 768, 256, 96, "y1")
        finish(256, 256)
        quantize_h("h1", 768, 256)
        tanh_quarter("h3", 3)
        park_y2(512, 256)
        park_y2(768, 256)
        gain_piece("h3", 768, 256, 144, "p1")
        multiply(512, 256)
        multiply(768, 256)
        quantize_h("h3", 768, 256)
        finish(512, 256)
        finish(768, 256, True)
